import numpy as np
import ml_dtypes


def mxq(x, axis, fmt="e4m3"):
    dtype, down = {"e4m3": (ml_dtypes.float8_e4m3fn, 7), "e5m2": (ml_dtypes.float8_e5m2, 14)}[fmt]
    v = np.moveaxis(np.asarray(x, np.float32).astype(ml_dtypes.bfloat16).astype(np.float64), axis, -1)
    blocks = v.reshape(v.shape[:-1] + (-1, 32))
    amax = np.abs(blocks).max(-1, keepdims=True)
    byte = np.maximum(np.where(amax > 0, np.frexp(amax)[1] - 1 + 127, 0) - down, 1)
    scale = np.exp2(byte - 127.0)
    codes = (blocks / scale).astype(np.float32).astype(dtype).astype(np.float64)
    return np.moveaxis((codes * scale).reshape(v.shape), -1, axis)


WIDE = False


def mx_kscale(k):
    if not WIDE:
        return np.ones(k)
    levels = np.array([10, -10, 5, -5, 0])
    if k % 512:
        return np.exp2(np.random.permutation(np.resize(levels, k // 32))).repeat(32)
    a = np.empty((k // 512, 16))
    for p in range(k // 512):
        a[p, :8] = np.random.permutation(np.resize(levels, 8))
        for g in range(8):
            far = levels[np.abs(levels - a[p, g]) >= 10]
            a[p, g + 8] = far[np.random.randint(len(far))]
    return np.exp2(a.ravel()).repeat(32)


def f64(x):
    return np.asarray(x).astype(np.float64)


def striped(idx):
    return np.tile(np.asarray(idx).reshape(-1, 16).T, (8, 1)).astype(np.uint16)


def unstriped(offs):
    return offs[:16].T.reshape(-1).astype(np.int64)


E2M1 = np.array([0.0, 0.5, 1.0, 1.5, 2.0, 3.0, 4.0, 6.0, -0.0, -0.5, -1.0, -1.5, -2.0, -3.0, -4.0, -6.0])


def pack_weight(w, fmt):
    k, n = w.shape
    w = f64(np.asarray(w, np.float32).astype(ml_dtypes.bfloat16)).reshape(k // 32, 32, n)
    amax = np.abs(w).max(1)
    if fmt == "e4m3":
        byte = np.frexp(amax)[1] - 1 + 127 - 7
    else:
        mant, ex = np.frexp(amax / 6.0)
        byte = np.where(mant > 0.5, ex, ex - 1) + 127
    byte = np.clip(np.where(amax > 0, byte, 1), 1, 254)
    scaled = (w * np.exp2(127.0 - byte)[:, None, :]).reshape(k, n).astype(np.float32)
    by_word = np.ascontiguousarray(scaled.reshape(k // 512, 128, 4, n).transpose(0, 1, 3, 2))
    if fmt == "e4m3":
        words = by_word.astype(ml_dtypes.float8_e4m3fn).view(np.uint8)
    else:
        c = by_word.astype(ml_dtypes.float4_e2m1fn).view(np.uint8) & 0xF
        words = (c[..., 0::2] | (c[..., 1::2] << 4)).reshape(k // 512, 128, 2 * n)
    return np.ascontiguousarray(words), np.ascontiguousarray(byte.astype(np.uint8).reshape(k // 512, 16, n))


def unpack_weight(words, scales, fmt):
    g, _, n = scales.shape
    words = np.ascontiguousarray(words).reshape(g, 128, n, -1)
    if fmt == "e4m3":
        vals = words.view(ml_dtypes.float8_e4m3fn).astype(np.float64)
    else:
        nib = np.empty((g, 128, n, 4), np.uint8)
        nib[..., 0::2] = words & 0xF
        nib[..., 1::2] = words >> 4
        vals = E2M1[nib]
    vals = vals * np.repeat(np.exp2(scales.astype(np.float64) - 127.0), 8, axis=1)[..., None]
    return vals.transpose(0, 1, 3, 2).reshape(g * 512, n)


def sigmoid(v):
    return 1.0 / (1.0 + np.exp(-v))


D, T, I, J, Q = 512, 2048, 1024, 512, 256


def setup_inputs():
    n = np.random.standard_normal
    idx = np.random.permutation(T)[:I]
    idx2 = np.random.randint(0, I, J)
    idx3 = np.random.randint(0, I, J)
    fd = mx_kscale(D)
    itemp = pack_weight(n((D, T)) / fd[:, None], "e2m1")
    return {
        "query": (n((D, Q)) * 0.8 / np.sqrt(D) * fd[:, None]).astype(np.float32),
        "item_words": itemp[0],
        "item_scales": itemp[1],
        "ib": np.tile(0.3 * n(T), (128, 1)).astype(np.float32),
        "offs": striped(idx),
        "offs2": striped(idx2),
        "offs3": striped(idx3),
    }


def reference(query, item_words, item_scales, ib, offs, offs2, offs3):
    idx = unstriped(offs)
    idx2 = unstriped(offs2)
    idx3 = unstriped(offs3)
    itemu = unpack_weight(item_words, item_scales, "e2m1")
    queryq = mxq(f64(query), 0, "e4m3")
    itemidxg = itemu[:, idx]
    a = queryq.T @ itemidxg
    s = a + f64(ib)[:1][:, idx]
    y = sigmoid(s[:, idx2] - s[:, idx3])
    return y

@@ -1,0 +1,109 @@
+from contextlib import ExitStack
+
+import concourse.mybir as mybir
+
+D, T, I, J, Q = 512, 2048, 1024, 512, 256
+FLOPS = 2 * D * I * Q
+
+F32 = mybir.dt.float32
+BF16 = mybir.dt.bfloat16
+I32 = mybir.dt.int32
+U32 = mybir.dt.uint32
+U16 = mybir.dt.uint16
+U8 = mybir.dt.uint8
+FP8X4 = mybir.dt.float8_e4m3fn_x4
+FP4X4 = mybir.dt.float4_e2m1fn_x4
+ACT = mybir.ActivationFunctionType
+ALU = mybir.AluOpType
+
+P = 128
+PACK = 4
+HALF = 512
+LANES = 16
+
+
+def tile_attend_pairprefs_kernel(tc, query, item_words, item_scales, ib, offs, offs2, offs3, out):
+    nc = tc.nc
+    with ExitStack() as ctx:
+        lists = ctx.enter_context(tc.tile_pool(name="lists", bufs=1))
+        keep = ctx.enter_context(tc.tile_pool(name="keep", bufs=1))
+        psum = ctx.enter_context(tc.psum_pool(name="psum", bufs=1))
+
+        slot_list = lists.tile([P, I // LANES], U16, name="slot_list")
+        first_list = lists.tile([P, J // LANES], U16, name="first_list")
+        second_list = lists.tile([P, J // LANES], U16, name="second_list")
+
+        scale_pool = keep.tile([P, T], U8, name="scale_pool", align_bytes=64)
+        word_pool = keep.tile([P, T], U16, name="word_pool", align_bytes=64)
+        bias_pool = keep.tile([P, T], F32, name="bias_pool", align_bytes=64)
+        q_raw = keep.tile([P, PACK, Q], F32, name="q_raw", align_bytes=64)
+
+        warm = keep.tile([P, 1], F32, name="warm")
+        warm_out = keep.tile([P, 1], F32, name="warm_out")
+        nc.gpsimd.memset(warm[:], 0.0)
+        nc.scalar.activation(warm_out[:], warm[:], ACT.Sigmoid)
+
+        nc.vector.memset(scale_pool[:].bitcast(I32), 0)
+        nc.sync.dma_start(slot_list[:], offs)
+        nc.sync.dma_start(word_pool[:].bitcast(I32), item_words[0].bitcast(I32))
+        for quad in range(4):
+            nc.scalar.dma_start(
+                scale_pool[32 * quad : 32 * quad + 4, :].bitcast(I32),
+                item_scales[0, 4 * quad : 4 * quad + 4, :].bitcast(I32),
+            )
+        nc.sync.dma_start(q_raw[:], query.rearrange("(p j) q -> p j q", j=PACK))
+        nc.sync.dma_start(bias_pool[:], ib)
+        nc.sync.dma_start(first_list[:], offs2)
+        nc.sync.dma_start(second_list[:], offs3)
+
+        q_grouped = keep.tile([P, Q, PACK], BF16, name="q_grouped", align_bytes=64)
+        nc.scalar.copy(q_grouped[:], q_raw[:].rearrange("p j q -> p q j"))
+        q_codes = keep.tile([P, Q], U32, name="q_codes", align_bytes=64)
+        q_scales = keep.tile([P, Q], U8, name="q_scales", align_bytes=64)
+
+        words, scales, biases = [], [], []
+        for h in range(I // HALF):
+            piece = slot_list[:, h * HALF // LANES : (h + 1) * HALF // LANES]
+            w = keep.tile([P, HALF], U16, name="words%d" % h, align_bytes=64)
+            nc.vector.tensor_copy(w[:], word_pool[:].indirect(piece))
+            s = keep.tile([P, HALF], U8, name="scales%d" % h, align_bytes=64)
+            nc.vector.tensor_copy(s[:], scale_pool[:].indirect(piece))
+            words.append(w)
+            scales.append(s)
+        nc.vector.quantize_mx(
+            out=q_codes[:].bitcast(FP8X4),
+            scales=q_scales[:],
+            in_=q_grouped[:].rearrange("p q j -> p (q j)"),
+        )
+        for h in range(I // HALF):
+            piece = slot_list[:, h * HALF // LANES : (h + 1) * HALF // LANES]
+            b = keep.tile([P, HALF], F32, name="biases%d" % h, align_bytes=64)
+            nc.vector.tensor_copy(b[:], bias_pool[:].indirect(piece))
+            biases.append(b)
+
+        for blk in range(Q // P):
+            cols = slice(blk * P, (blk + 1) * P)
+            score = keep.tile([P, I], F32, name="score%d" % blk, align_bytes=64)
+            for h in range(I // HALF):
+                acc = psum.tile([P, HALF], F32, name="acc%d_%d" % (blk, h))
+                nc.tensor.matmul_mx(
+                    out=acc[:],
+                    lhsT=q_codes[:, cols].bitcast(FP8X4),
+                    lhsT_scale=q_scales[:, cols],
+                    rhs=words[h][:].bitcast(FP4X4),
+                    rhs_scale=scales[h][:],
+                    start=True,
+                    stop=True,
+                )
+                nc.vector.tensor_tensor(score[:, h * HALF : (h + 1) * HALF], acc[:], biases[h][:], ALU.add)
+            second = keep.tile([P, J], F32, name="second%d" % blk, align_bytes=64)
+            nc.vector.tensor_copy(second[:], score[:].indirect(second_list[:]))
+            pieces = [(0, J)] if blk == 0 else [(0, 384), (384, J)]
+            for lo, hi in pieces:
+                diff = keep.tile([P, hi - lo], F32, name="diff%d_%d" % (blk, lo), align_bytes=64)
+                nc.vector.tensor_tensor(
+                    diff[:], score[:].indirect(first_list[:, lo // LANES : hi // LANES]), second[:, lo:hi], ALU.subtract
+                )
+                res = keep.tile([P, hi - lo], F32, name="res%d_%d" % (blk, lo), align_bytes=64)
+                nc.scalar.activation(res[:], diff[:], ACT.Sigmoid)
+                nc.sync.dma_start(out[cols, lo:hi], res[:])

@@ -1,6 +1,7 @@
 from contextlib import ExitStack
 
 import concourse.mybir as mybir
+from concourse.masks import make_identity
 
 D, T, I, J, Q = 512, 2048, 1024, 512, 256
 FLOPS = 2 * D * I * Q
@@ -20,6 +21,7 @@ P = 128
 PACK = 4
 HALF = 512
 LANES = 16
+BLOCKS = HALF // P
 
 
 def tile_attend_pairprefs_kernel(tc, query, item_words, item_scales, ib, offs, offs2, offs3, out):
@@ -33,77 +35,137 @@ def tile_attend_pairprefs_kernel(tc, query, item_words, item_scales, ib, offs, o
         first_list = lists.tile([P, J // LANES], U16, name="first_list")
         second_list = lists.tile([P, J // LANES], U16, name="second_list")
 
-        scale_pool = keep.tile([P, T], U8, name="scale_pool", align_bytes=64)
-        word_pool = keep.tile([P, T], U16, name="word_pool", align_bytes=64)
+        scale_pool = keep.tile([P, T], U8, name="scale_pool", tag="scales_then_words", align_bytes=64)
+        word_pool = keep.tile([P, T], U16, name="word_pool", tag="words_then_biases", align_bytes=64)
+        bias_rows = keep.tile([P, T], F32, name="bias_rows", align_bytes=64)
         bias_pool = keep.tile([P, T], F32, name="bias_pool", align_bytes=64)
-        q_raw = keep.tile([P, PACK, Q], F32, name="q_raw", align_bytes=64)
+        q_raw = keep.tile([P, PACK, Q], F32, name="q_raw", tag="query_then_columns", align_bytes=64)
 
-        warm = keep.tile([P, 1], F32, name="warm")
-        warm_out = keep.tile([P, 1], F32, name="warm_out")
-        nc.gpsimd.memset(warm[:], 0.0)
-        nc.scalar.activation(warm_out[:], warm[:], ACT.Sigmoid)
+        ident = keep.tile([P, P], F32, name="ident", align_bytes=64)
+        make_identity(nc, ident[:])
 
         nc.vector.memset(scale_pool[:].bitcast(I32), 0)
-        nc.sync.dma_start(slot_list[:], offs)
+        nc.vector.memset(bias_rows[0:96, :].bitcast(I32), 0)
         nc.sync.dma_start(word_pool[:].bitcast(I32), item_words[0].bitcast(I32))
+        nc.sync.dma_start(slot_list[:], offs)
+        nc.sync.dma_start(bias_rows[96:P, :], ib[96:P, :])
         for quad in range(4):
-            nc.scalar.dma_start(
+            nc.sync.dma_start(
                 scale_pool[32 * quad : 32 * quad + 4, :].bitcast(I32),
                 item_scales[0, 4 * quad : 4 * quad + 4, :].bitcast(I32),
             )
         nc.sync.dma_start(q_raw[:], query.rearrange("(p j) q -> p j q", j=PACK))
         nc.sync.dma_start(bias_pool[:], ib)
-        nc.sync.dma_start(first_list[:], offs2)
         nc.sync.dma_start(second_list[:], offs3)
+        nc.sync.dma_start(first_list[:], offs2)
 
-        q_grouped = keep.tile([P, Q, PACK], BF16, name="q_grouped", align_bytes=64)
-        nc.scalar.copy(q_grouped[:], q_raw[:].rearrange("p j q -> p q j"))
-        q_codes = keep.tile([P, Q], U32, name="q_codes", align_bytes=64)
-        q_scales = keep.tile([P, Q], U8, name="q_scales", align_bytes=64)
+        def group(blk, tag):
+            grouped = keep.tile([P, P, PACK], BF16, name="q_grouped%d" % blk, tag=tag, align_bytes=64)
+            nc.scalar.copy(grouped[:], q_raw[:, :, blk * P : (blk + 1) * P].rearrange("p j q -> p q j"))
+            return grouped
 
-        words, scales, biases = [], [], []
-        for h in range(I // HALF):
+        def quantize(grouped, blk):
+            codes = keep.tile([P, P], U32, name="q_codes%d" % blk, align_bytes=64)
+            scales = keep.tile([P, P], U8, name="q_scales%d" % blk, align_bytes=64)
+            nc.vector.quantize_mx(
+                out=codes[:].bitcast(FP8X4), scales=scales[:], in_=grouped[:].rearrange("p q j -> p (q j)")
+            )
+            return codes, scales
+
+        def gather(dtype, window, h, name, tag):
+            got = keep.tile([P, HALF], dtype, name=name, tag=tag, align_bytes=64)
             piece = slot_list[:, h * HALF // LANES : (h + 1) * HALF // LANES]
-            w = keep.tile([P, HALF], U16, name="words%d" % h, align_bytes=64)
-            nc.vector.tensor_copy(w[:], word_pool[:].indirect(piece))
-            s = keep.tile([P, HALF], U8, name="scales%d" % h, align_bytes=64)
-            nc.vector.tensor_copy(s[:], scale_pool[:].indirect(piece))
-            words.append(w)
-            scales.append(s)
-        nc.vector.quantize_mx(
-            out=q_codes[:].bitcast(FP8X4),
-            scales=q_scales[:],
-            in_=q_grouped[:].rearrange("p q j -> p (q j)"),
-        )
-        for h in range(I // HALF):
-            piece = slot_list[:, h * HALF // LANES : (h + 1) * HALF // LANES]
-            b = keep.tile([P, HALF], F32, name="biases%d" % h, align_bytes=64)
-            nc.vector.tensor_copy(b[:], bias_pool[:].indirect(piece))
-            biases.append(b)
+            nc.vector.tensor_copy(got[:], window[:].indirect(piece))
+            return got
 
-        for blk in range(Q // P):
-            cols = slice(blk * P, (blk + 1) * P)
-            score = keep.tile([P, I], F32, name="score%d" % blk, align_bytes=64)
-            for h in range(I // HALF):
-                acc = psum.tile([P, HALF], F32, name="acc%d_%d" % (blk, h))
+        grouped = [group(0, "q_grouped0"), group(1, "query_then_scales")]
+        words0 = gather(U16, word_pool, 0, "words0", "words0")
+        biases0 = gather(F32, bias_rows, 0, "biases0", "biases0")
+        scales0 = gather(U8, scale_pool, 0, "scales0", "scales0")
+        users = [quantize(grouped[blk], blk) for blk in range(2)]
+        scales1 = gather(U8, scale_pool, 1, "scales1", "query_then_scales")
+        words1 = gather(U16, word_pool, 1, "words1", "scales_then_words")
+        biases1 = keep.tile([P, HALF], F32, name="biases1", tag="words_then_biases", align_bytes=64)
+        for lo in (0, HALF // 2):
+            piece = slot_list[:, (HALF + lo) // LANES : (HALF + lo + HALF // 2) // LANES]
+            nc.vector.tensor_copy(biases1[:, lo : lo + HALF // 2], bias_pool[:].indirect(piece))
+
+        score = [keep.tile([P, I], F32, name="score%d" % blk, align_bytes=64) for blk in range(2)]
+
+        turned = psum.tile([P, BLOCKS, P], F32, name="turned")
+        for c in range(BLOCKS):
+            nc.tensor.transpose(turned[:, c, :], biases0[:, c * P : (c + 1) * P], ident[:])
+        columns = keep.tile([P, BLOCKS], F32, name="columns", tag="query_then_columns", align_bytes=64)
+        nc.scalar.copy(columns[:], turned[:, :, 96])
+
+        accs = []
+        for blk in range(2):
+            acc = psum.tile([P, BLOCKS, P], F32, name="acc%d" % blk, tag="acc%d" % blk)
+            for c in range(BLOCKS):
+                slots = slice(c * P, (c + 1) * P)
                 nc.tensor.matmul_mx(
-                    out=acc[:],
-                    lhsT=q_codes[:, cols].bitcast(FP8X4),
-                    lhsT_scale=q_scales[:, cols],
-                    rhs=words[h][:].bitcast(FP4X4),
-                    rhs_scale=scales[h][:],
+                    out=acc[:, c, :],
+                    lhsT=words0[:, slots].bitcast(FP4X4),
+                    lhsT_scale=scales0[:, slots],
+                    rhs=users[blk][0][:].bitcast(FP8X4),
+                    rhs_scale=users[blk][1][:],
                     start=True,
                     stop=True,
                 )
-                nc.vector.tensor_tensor(score[:, h * HALF : (h + 1) * HALF], acc[:], biases[h][:], ALU.add)
-            second = keep.tile([P, J], F32, name="second%d" % blk, align_bytes=64)
-            nc.vector.tensor_copy(second[:], score[:].indirect(second_list[:]))
-            pieces = [(0, J)] if blk == 0 else [(0, 384), (384, J)]
-            for lo, hi in pieces:
-                diff = keep.tile([P, hi - lo], F32, name="diff%d_%d" % (blk, lo), align_bytes=64)
+            accs.append(acc)
+
+        def add_bias(blk):
+            biased = keep.tile([P, BLOCKS, P], F32, name="biased%d" % blk, align_bytes=64)
+            for c in range(BLOCKS):
+                nc.scalar.activation(biased[:, c, :], accs[blk][:, c, :], ACT.Identity, bias=columns[:, c : c + 1])
+            return biased
+
+        def turn_back(biased, blk):
+            back = psum.tile([P, HALF], F32, name="back%d" % blk, tag="back%d" % blk)
+            for c in range(BLOCKS):
+                nc.tensor.transpose(back[:, c * P : (c + 1) * P], biased[:, c, :], ident[:])
+            nc.scalar.copy(score[blk][:, 0:HALF], back[:])
+
+        def direct_half(blk, tag):
+            direct = psum.tile([P, HALF], F32, name="direct%d" % blk, tag=tag)
+            nc.tensor.matmul_mx(
+                out=direct[:],
+                lhsT=users[blk][0][:].bitcast(FP8X4),
+                lhsT_scale=users[blk][1][:],
+                rhs=words1[:].bitcast(FP4X4),
+                rhs_scale=scales1[:],
+                start=True,
+                stop=True,
+            )
+            width = HALF // 2 if blk == 0 else HALF
+            for lo in range(0, HALF, width):
                 nc.vector.tensor_tensor(
-                    diff[:], score[:].indirect(first_list[:, lo // LANES : hi // LANES]), second[:, lo:hi], ALU.subtract
+                    score[blk][:, HALF + lo : HALF + lo + width],
+                    direct[:, lo : lo + width],
+                    biases1[:, lo : lo + width],
+                    ALU.add,
                 )
-                res = keep.tile([P, hi - lo], F32, name="res%d_%d" % (blk, lo), align_bytes=64)
-                nc.scalar.activation(res[:], diff[:], ACT.Sigmoid)
-                nc.sync.dma_start(out[cols, lo:hi], res[:])
+
+        biased0 = add_bias(0)
+        biased1 = add_bias(1)
+        turn_back(biased0, 0)
+        turn_back(biased1, 1)
+        direct_half(0, "acc1")
+        direct_half(1, "back0")
+
+        seconds = []
+        for blk in range(2):
+            second = keep.tile([P, J], F32, name="second%d" % blk, align_bytes=64)
+            nc.vector.tensor_copy(second[:], score[blk][:].indirect(second_list[:]))
+            seconds.append(second)
+        for blk, lo, hi in [(0, 0, J), (1, 0, 384), (1, 384, J)]:
+            diff = keep.tile([P, hi - lo], F32, name="diff%d_%d" % (blk, lo), align_bytes=64)
+            nc.vector.tensor_tensor(
+                diff[:],
+                score[blk][:].indirect(first_list[:, lo // LANES : hi // LANES]),
+                seconds[blk][:, lo:hi],
+                ALU.subtract,
+            )
+            res = keep.tile([P, hi - lo], F32, name="res%d_%d" % (blk, lo), align_bytes=64)
+            nc.scalar.activation(res[:], diff[:], ACT.Sigmoid)
+            nc.sync.dma_start(out[blk * P : (blk + 1) * P, lo:hi], res[:])

@@ -19,9 +19,13 @@ ALU = mybir.AluOpType
 
 P = 128
 PACK = 4
-HALF = 512
+QUADRANT = 32
+LAST_QUADRANT = P - QUADRANT
 LANES = 16
-BLOCKS = HALF // P
+HALF = I // 2
+QUARTER = HALF // 2
+SLOT_TILES = HALF // P
+PAIR_PIECES = [(256, 256), (256, 128, 128)]
 
 
 def tile_attend_pairprefs_kernel(tc, query, item_words, item_scales, ib, offs, offs2, offs3, out):
@@ -35,7 +39,7 @@ def tile_attend_pairprefs_kernel(tc, query, item_words, item_scales, ib, offs, o
         first_list = lists.tile([P, J // LANES], U16, name="first_list")
         second_list = lists.tile([P, J // LANES], U16, name="second_list")
 
-        scale_pool = keep.tile([P, T], U8, name="scale_pool", tag="scales_then_words", align_bytes=64)
+        scale_pool = keep.tile([P, T], U8, name="scale_pool", align_bytes=64)
         word_pool = keep.tile([P, T], U16, name="word_pool", tag="words_then_biases", align_bytes=64)
         bias_rows = keep.tile([P, T], F32, name="bias_rows", align_bytes=64)
         bias_pool = keep.tile([P, T], F32, name="bias_pool", align_bytes=64)
@@ -45,63 +49,66 @@ def tile_attend_pairprefs_kernel(tc, query, item_words, item_scales, ib, offs, o
         make_identity(nc, ident[:])
 
         nc.vector.memset(scale_pool[:].bitcast(I32), 0)
-        nc.vector.memset(bias_rows[0:96, :].bitcast(I32), 0)
+        nc.vector.memset(bias_rows[0:LAST_QUADRANT, :].bitcast(I32), 0)
         nc.sync.dma_start(word_pool[:].bitcast(I32), item_words[0].bitcast(I32))
         nc.sync.dma_start(slot_list[:], offs)
-        nc.sync.dma_start(bias_rows[96:P, :], ib[96:P, :])
-        for quad in range(4):
+        nc.sync.dma_start(bias_rows[LAST_QUADRANT:P, :], ib[LAST_QUADRANT:P, :])
+        for quad in range(P // QUADRANT):
             nc.sync.dma_start(
-                scale_pool[32 * quad : 32 * quad + 4, :].bitcast(I32),
-                item_scales[0, 4 * quad : 4 * quad + 4, :].bitcast(I32),
+                scale_pool[QUADRANT * quad : QUADRANT * quad + PACK, :].bitcast(I32),
+                item_scales[0, PACK * quad : PACK * quad + PACK, :].bitcast(I32),
             )
-        nc.sync.dma_start(q_raw[:], query.rearrange("(p j) q -> p j q", j=PACK))
+        nc.sync.dma_start(q_raw[:], query.rearrange("(p t) q -> p t q", t=PACK))
         nc.sync.dma_start(bias_pool[:], ib)
         nc.sync.dma_start(second_list[:], offs3)
         nc.sync.dma_start(first_list[:], offs2)
 
         def group(blk, tag):
             grouped = keep.tile([P, P, PACK], BF16, name="q_grouped%d" % blk, tag=tag, align_bytes=64)
-            nc.scalar.copy(grouped[:], q_raw[:, :, blk * P : (blk + 1) * P].rearrange("p j q -> p q j"))
+            nc.scalar.copy(
+                grouped[:].rearrange("p (c i) t -> p c t i", i=PACK),
+                q_raw[:, :, blk * P : (blk + 1) * P].rearrange("p t (c i) -> p c t i", i=PACK),
+            )
             return grouped
 
         def quantize(grouped, blk):
             codes = keep.tile([P, P], U32, name="q_codes%d" % blk, align_bytes=64)
             scales = keep.tile([P, P], U8, name="q_scales%d" % blk, align_bytes=64)
             nc.vector.quantize_mx(
-                out=codes[:].bitcast(FP8X4), scales=scales[:], in_=grouped[:].rearrange("p q j -> p (q j)")
+                out=codes[:].bitcast(FP8X4), scales=scales[:], in_=grouped[:].rearrange("p q t -> p (q t)")
             )
             return codes, scales
 
-        def gather(dtype, window, h, name, tag):
+        def gather(dtype, window, half, name, tag):
             got = keep.tile([P, HALF], dtype, name=name, tag=tag, align_bytes=64)
-            piece = slot_list[:, h * HALF // LANES : (h + 1) * HALF // LANES]
-            nc.vector.tensor_copy(got[:], window[:].indirect(piece))
+            entries = slot_list[:, half * HALF // LANES : (half + 1) * HALF // LANES]
+            nc.vector.tensor_copy(got[:], window[:].indirect(entries))
             return got
 
-        grouped = [group(0, "q_grouped0"), group(1, "query_then_scales")]
+        grouped = [group(0, "query_then_scales"), group(1, "query_then_words")]
         words0 = gather(U16, word_pool, 0, "words0", "words0")
         biases0 = gather(F32, bias_rows, 0, "biases0", "biases0")
         scales0 = gather(U8, scale_pool, 0, "scales0", "scales0")
-        users = [quantize(grouped[blk], blk) for blk in range(2)]
+        users = [quantize(grouped[0], 0)]
         scales1 = gather(U8, scale_pool, 1, "scales1", "query_then_scales")
-        words1 = gather(U16, word_pool, 1, "words1", "scales_then_words")
+        users.append(quantize(grouped[1], 1))
+        words1 = gather(U16, word_pool, 1, "words1", "query_then_words")
         biases1 = keep.tile([P, HALF], F32, name="biases1", tag="words_then_biases", align_bytes=64)
-        for lo in (0, HALF // 2):
-            piece = slot_list[:, (HALF + lo) // LANES : (HALF + lo + HALF // 2) // LANES]
-            nc.vector.tensor_copy(biases1[:, lo : lo + HALF // 2], bias_pool[:].indirect(piece))
+        for lo in (0, QUARTER):
+            entries = slot_list[:, (HALF + lo) // LANES : (HALF + lo + QUARTER) // LANES]
+            nc.vector.tensor_copy(biases1[:, lo : lo + QUARTER], bias_pool[:].indirect(entries))
 
-        score = [keep.tile([P, I], F32, name="score%d" % blk, align_bytes=64) for blk in range(2)]
+        score = [keep.tile([P, I], F32, name="score%d" % blk, align_bytes=64) for blk in range(Q // P)]
 
-        turned = psum.tile([P, BLOCKS, P], F32, name="turned")
-        for c in range(BLOCKS):
+        turned = psum.tile([P, SLOT_TILES, P], F32, name="turned")
+        for c in range(SLOT_TILES):
             nc.tensor.transpose(turned[:, c, :], biases0[:, c * P : (c + 1) * P], ident[:])
-        columns = keep.tile([P, BLOCKS], F32, name="columns", tag="query_then_columns", align_bytes=64)
-        nc.scalar.copy(columns[:], turned[:, :, 96])
+        columns = keep.tile([P, SLOT_TILES], F32, name="columns", tag="query_then_columns", align_bytes=64)
+        nc.scalar.copy(columns[:], turned[:, :, LAST_QUADRANT])
 
-        accs = []
-        for blk in range(2):
-            acc = psum.tile([P, BLOCKS, P], F32, name="acc%d" % blk, tag="acc%d" % blk)
-            for c in range(BLOCKS):
+        def biased_products(blk):
+            acc = psum.tile([P, SLOT_TILES, P], F32, name="acc%d" % blk, tag="acc")
+            for c in range(SLOT_TILES):
                 slots = slice(c * P, (c + 1) * P)
                 nc.tensor.matmul_mx(
                     out=acc[:, c, :],
@@ -112,21 +119,18 @@ def tile_attend_pairprefs_kernel(tc, query, item_words, item_scales, ib, offs, o
                     start=True,
                     stop=True,
                 )
-            accs.append(acc)
-
-        def add_bias(blk):
-            biased = keep.tile([P, BLOCKS, P], F32, name="biased%d" % blk, align_bytes=64)
-            for c in range(BLOCKS):
-                nc.scalar.activation(biased[:, c, :], accs[blk][:, c, :], ACT.Identity, bias=columns[:, c : c + 1])
+            biased = keep.tile([P, SLOT_TILES, P], F32, name="biased%d" % blk, align_bytes=64)
+            for c in range(SLOT_TILES):
+                nc.scalar.activation(biased[:, c, :], acc[:, c, :], ACT.Identity, bias=columns[:, c : c + 1])
             return biased
 
-        def turn_back(biased, blk):
-            back = psum.tile([P, HALF], F32, name="back%d" % blk, tag="back%d" % blk)
-            for c in range(BLOCKS):
-                nc.tensor.transpose(back[:, c * P : (c + 1) * P], biased[:, c, :], ident[:])
-            nc.scalar.copy(score[blk][:, 0:HALF], back[:])
+        def turn_back(biased, blk, first, count, tag):
+            back = psum.tile([P, count, P], F32, name="back%d_%d" % (blk, first), tag=tag)
+            for c in range(count):
+                nc.tensor.transpose(back[:, c, :], biased[:, first + c, :], ident[:])
+            nc.scalar.copy(score[blk][:, first * P : (first + count) * P], back[:].rearrange("p c q -> p (c q)"))
 
-        def direct_half(blk, tag):
+        def direct_half(blk, tag, width):
             direct = psum.tile([P, HALF], F32, name="direct%d" % blk, tag=tag)
             nc.tensor.matmul_mx(
                 out=direct[:],
@@ -137,7 +141,6 @@ def tile_attend_pairprefs_kernel(tc, query, item_words, item_scales, ib, offs, o
                 start=True,
                 stop=True,
             )
-            width = HALF // 2 if blk == 0 else HALF
             for lo in range(0, HALF, width):
                 nc.vector.tensor_tensor(
                     score[blk][:, HALF + lo : HALF + lo + width],
@@ -146,26 +149,30 @@ def tile_attend_pairprefs_kernel(tc, query, item_words, item_scales, ib, offs, o
                     ALU.add,
                 )
 
-        biased0 = add_bias(0)
-        biased1 = add_bias(1)
-        turn_back(biased0, 0)
-        turn_back(biased1, 1)
-        direct_half(0, "acc1")
-        direct_half(1, "back0")
+        biased0 = biased_products(0)
+        turn_back(biased0, 0, 0, SLOT_TILES // 2, "bank_a")
+        turn_back(biased0, 0, SLOT_TILES // 2, SLOT_TILES // 2, "bank_b")
+        biased1 = biased_products(1)
+        direct_half(0, "bank_a", QUARTER)
+        direct_half(1, "bank_b", HALF)
+        turn_back(biased1, 1, 0, SLOT_TILES, "bank_c")
 
-        seconds = []
-        for blk in range(2):
+        for blk, widths in enumerate(PAIR_PIECES):
             second = keep.tile([P, J], F32, name="second%d" % blk, align_bytes=64)
-            nc.vector.tensor_copy(second[:], score[blk][:].indirect(second_list[:]))
-            seconds.append(second)
-        for blk, lo, hi in [(0, 0, J), (1, 0, 384), (1, 384, J)]:
-            diff = keep.tile([P, hi - lo], F32, name="diff%d_%d" % (blk, lo), align_bytes=64)
-            nc.vector.tensor_tensor(
-                diff[:],
-                score[blk][:].indirect(first_list[:, lo // LANES : hi // LANES]),
-                seconds[blk][:, lo:hi],
-                ALU.subtract,
-            )
-            res = keep.tile([P, hi - lo], F32, name="res%d_%d" % (blk, lo), align_bytes=64)
-            nc.scalar.activation(res[:], diff[:], ACT.Sigmoid)
-            nc.sync.dma_start(out[blk * P : (blk + 1) * P, lo:hi], res[:])
+            for lo in (0, J // 2):
+                entries = second_list[:, lo // LANES : (lo + J // 2) // LANES]
+                nc.vector.tensor_copy(second[:, lo : lo + J // 2], score[blk][:].indirect(entries))
+            lo = 0
+            for width in widths:
+                hi = lo + width
+                diff = keep.tile([P, width], F32, name="diff%d_%d" % (blk, lo), align_bytes=64)
+                nc.vector.tensor_tensor(
+                    diff[:],
+                    score[blk][:].indirect(first_list[:, lo // LANES : hi // LANES]),
+                    second[:, lo:hi],
+                    ALU.subtract,
+                )
+                result = keep.tile([P, width], F32, name="result%d_%d" % (blk, lo), align_bytes=64)
+                nc.scalar.activation(result[:], diff[:], ACT.Sigmoid)
+                nc.sync.dma_start(out[blk * P : (blk + 1) * P, lo:hi], result[:])
+                lo = hi

@@ -20,7 +20,7 @@ ALU = mybir.AluOpType
 P = 128
 PACK = 4
 QUADRANT = 32
-LAST_QUADRANT = P - QUADRANT
+LAST = P - 1
 LANES = 16
 HALF = I // 2
 QUARTER = HALF // 2
@@ -33,6 +33,7 @@ def tile_attend_pairprefs_kernel(tc, query, item_words, item_scales, ib, offs, o
     with ExitStack() as ctx:
         lists = ctx.enter_context(tc.tile_pool(name="lists", bufs=1))
         keep = ctx.enter_context(tc.tile_pool(name="keep", bufs=1))
+        reused = ctx.enter_context(tc.tile_pool(name="reused", bufs=1))
         psum = ctx.enter_context(tc.psum_pool(name="psum", bufs=1))
 
         slot_list = lists.tile([P, I // LANES], U16, name="slot_list")
@@ -40,19 +41,19 @@ def tile_attend_pairprefs_kernel(tc, query, item_words, item_scales, ib, offs, o
         second_list = lists.tile([P, J // LANES], U16, name="second_list")
 
         scale_pool = keep.tile([P, T], U8, name="scale_pool", align_bytes=64)
-        word_pool = keep.tile([P, T], U16, name="word_pool", tag="words_then_biases", align_bytes=64)
-        bias_rows = keep.tile([P, T], F32, name="bias_rows", align_bytes=64)
+        word_pool = keep.tile([P, T], U16, name="word_pool", align_bytes=64)
+        bias_row = keep.tile([P, T], F32, name="bias_row", align_bytes=64)
         bias_pool = keep.tile([P, T], F32, name="bias_pool", align_bytes=64)
-        q_raw = keep.tile([P, PACK, Q], F32, name="q_raw", tag="query_then_columns", align_bytes=64)
+        q_raw = reused.tile([P, PACK, Q], F32, name="q_raw", align_bytes=64, offset=0)
 
+        nc.gpsimd.memset(scale_pool[:].bitcast(I32), 0)
         ident = keep.tile([P, P], F32, name="ident", align_bytes=64)
         make_identity(nc, ident[:])
 
-        nc.vector.memset(scale_pool[:].bitcast(I32), 0)
-        nc.vector.memset(bias_rows[0:LAST_QUADRANT, :].bitcast(I32), 0)
-        nc.sync.dma_start(word_pool[:].bitcast(I32), item_words[0].bitcast(I32))
+        nc.vector.memset(bias_row[0:LAST, :].bitcast(I32), 0)
         nc.sync.dma_start(slot_list[:], offs)
-        nc.sync.dma_start(bias_rows[LAST_QUADRANT:P, :], ib[LAST_QUADRANT:P, :])
+        nc.sync.dma_start(bias_row[LAST:P, :], ib[LAST:P, :])
+        nc.sync.dma_start(word_pool[:].bitcast(I32), item_words[0].bitcast(I32))
         for quad in range(P // QUADRANT):
             nc.sync.dma_start(
                 scale_pool[QUADRANT * quad : QUADRANT * quad + PACK, :].bitcast(I32),
@@ -63,99 +64,120 @@ def tile_attend_pairprefs_kernel(tc, query, item_words, item_scales, ib, offs, o
         nc.sync.dma_start(second_list[:], offs3)
         nc.sync.dma_start(first_list[:], offs2)
 
-        def group(blk, tag):
-            grouped = keep.tile([P, P, PACK], BF16, name="q_grouped%d" % blk, tag=tag, align_bytes=64)
+        warm = keep.tile([P, 1], F32, name="warm", align_bytes=64)
+        nc.scalar.activation(warm[:], ident[:, 0:1], ACT.Sigmoid)
+
+        grouped = keep.tile([P, Q, PACK], BF16, name="grouped", align_bytes=64)
+        for blk in range(Q // P):
             nc.scalar.copy(
-                grouped[:].rearrange("p (c i) t -> p c t i", i=PACK),
+                grouped[:, blk * P : (blk + 1) * P, :].rearrange("p (c i) t -> p c t i", i=PACK),
                 q_raw[:, :, blk * P : (blk + 1) * P].rearrange("p t (c i) -> p c t i", i=PACK),
             )
-            return grouped
 
-        def quantize(grouped, blk):
-            codes = keep.tile([P, P], U32, name="q_codes%d" % blk, align_bytes=64)
-            scales = keep.tile([P, P], U8, name="q_scales%d" % blk, align_bytes=64)
+        def quantize(blk):
+            users = slice(blk * P, (blk + 1) * P)
             nc.vector.quantize_mx(
-                out=codes[:].bitcast(FP8X4), scales=scales[:], in_=grouped[:].rearrange("p q t -> p (q t)")
+                out=q_codes[:, users].bitcast(FP8X4),
+                scales=q_scales[:, users],
+                in_=grouped[:, users, :].rearrange("p q t -> p (q t)"),
             )
-            return codes, scales
 
-        def gather(dtype, window, half, name, tag):
-            got = keep.tile([P, HALF], dtype, name=name, tag=tag, align_bytes=64)
-            entries = slot_list[:, half * HALF // LANES : (half + 1) * HALF // LANES]
-            nc.vector.tensor_copy(got[:], window[:].indirect(entries))
-            return got
+        def gather(got, window, lo, hi):
+            nc.vector.tensor_copy(got, window[:].indirect(slot_list[:, lo // LANES : hi // LANES]))
 
-        grouped = [group(0, "query_then_scales"), group(1, "query_then_words")]
-        words0 = gather(U16, word_pool, 0, "words0", "words0")
-        biases0 = gather(F32, bias_rows, 0, "biases0", "biases0")
-        scales0 = gather(U8, scale_pool, 0, "scales0", "scales0")
-        users = [quantize(grouped[0], 0)]
-        scales1 = gather(U8, scale_pool, 1, "scales1", "query_then_scales")
-        users.append(quantize(grouped[1], 1))
-        words1 = gather(U16, word_pool, 1, "words1", "query_then_words")
-        biases1 = keep.tile([P, HALF], F32, name="biases1", tag="words_then_biases", align_bytes=64)
+        biases0 = keep.tile([P, HALF], F32, name="biases0", align_bytes=64)
+        words0 = keep.tile([P, HALF], U16, name="words0", align_bytes=64)
+        scales0 = keep.tile([P, HALF], U8, name="scales0", align_bytes=64)
+        words1 = [
+            keep.tile([P, QUARTER], U16, name="words1a", align_bytes=64),
+            reused.tile([P, QUARTER], U16, name="words1b", align_bytes=64, offset=2624),
+        ]
+        scales1 = reused.tile([P, HALF], U8, name="scales1", align_bytes=64, offset=0)
+        biases1 = reused.tile([P, HALF], F32, name="biases1", align_bytes=64, offset=512)
+        columns = reused.tile([P, SLOT_TILES], F32, name="columns", align_bytes=64, offset=2560)
+        q_codes = keep.tile([P, Q], U32, name="q_codes", align_bytes=64)
+        q_scales = keep.tile([P, Q], U8, name="q_scales", align_bytes=64)
+
+        gather(biases0[:], bias_row, 0, HALF)
+        gather(words0[:], word_pool, 0, HALF)
+        gather(scales0[:], scale_pool, 0, HALF)
+        gather(words1[0][:], word_pool, HALF, HALF + QUARTER)
+        quantize(0)
+        gather(words1[1][:], word_pool, HALF + QUARTER, I)
+        quantize(1)
+        gather(scales1[:], scale_pool, HALF, I)
         for lo in (0, QUARTER):
-            entries = slot_list[:, (HALF + lo) // LANES : (HALF + lo + QUARTER) // LANES]
-            nc.vector.tensor_copy(biases1[:, lo : lo + QUARTER], bias_pool[:].indirect(entries))
+            gather(biases1[:, lo : lo + QUARTER], bias_pool, HALF + lo, HALF + lo + QUARTER)
 
         score = [keep.tile([P, I], F32, name="score%d" % blk, align_bytes=64) for blk in range(Q // P)]
 
         turned = psum.tile([P, SLOT_TILES, P], F32, name="turned")
         for c in range(SLOT_TILES):
             nc.tensor.transpose(turned[:, c, :], biases0[:, c * P : (c + 1) * P], ident[:])
-        columns = keep.tile([P, SLOT_TILES], F32, name="columns", tag="query_then_columns", align_bytes=64)
-        nc.scalar.copy(columns[:], turned[:, :, LAST_QUADRANT])
+        nc.scalar.copy(columns[:], turned[:, :, LAST])
 
-        def biased_products(blk):
-            acc = psum.tile([P, SLOT_TILES, P], F32, name="acc%d" % blk, tag="acc")
-            for c in range(SLOT_TILES):
-                slots = slice(c * P, (c + 1) * P)
+        def biased_products(blk, biased, first, count, tag):
+            users = slice(blk * P, (blk + 1) * P)
+            acc = psum.tile([P, count, P], F32, name="acc%d_%d" % (blk, first), tag=tag)
+            for c in range(count):
+                slots = slice((first + c) * P, (first + c + 1) * P)
                 nc.tensor.matmul_mx(
                     out=acc[:, c, :],
                     lhsT=words0[:, slots].bitcast(FP4X4),
                     lhsT_scale=scales0[:, slots],
-                    rhs=users[blk][0][:].bitcast(FP8X4),
-                    rhs_scale=users[blk][1][:],
+                    rhs=q_codes[:, users].bitcast(FP8X4),
+                    rhs_scale=q_scales[:, users],
                     start=True,
                     stop=True,
                 )
-            biased = keep.tile([P, SLOT_TILES, P], F32, name="biased%d" % blk, align_bytes=64)
-            for c in range(SLOT_TILES):
-                nc.scalar.activation(biased[:, c, :], acc[:, c, :], ACT.Identity, bias=columns[:, c : c + 1])
-            return biased
-
-        def turn_back(biased, blk, first, count, tag):
-            back = psum.tile([P, count, P], F32, name="back%d_%d" % (blk, first), tag=tag)
             for c in range(count):
-                nc.tensor.transpose(back[:, c, :], biased[:, first + c, :], ident[:])
-            nc.scalar.copy(score[blk][:, first * P : (first + count) * P], back[:].rearrange("p c q -> p (c q)"))
-
-        def direct_half(blk, tag, width):
-            direct = psum.tile([P, HALF], F32, name="direct%d" % blk, tag=tag)
-            nc.tensor.matmul_mx(
-                out=direct[:],
-                lhsT=users[blk][0][:].bitcast(FP8X4),
-                lhsT_scale=users[blk][1][:],
-                rhs=words1[:].bitcast(FP4X4),
-                rhs_scale=scales1[:],
-                start=True,
-                stop=True,
-            )
-            for lo in range(0, HALF, width):
-                nc.vector.tensor_tensor(
-                    score[blk][:, HALF + lo : HALF + lo + width],
-                    direct[:, lo : lo + width],
-                    biases1[:, lo : lo + width],
-                    ALU.add,
+                nc.scalar.activation(
+                    biased[:, first + c, :], acc[:, c, :], ACT.Identity, bias=columns[:, first + c : first + c + 1]
                 )
 
-        biased0 = biased_products(0)
-        turn_back(biased0, 0, 0, SLOT_TILES // 2, "bank_a")
-        turn_back(biased0, 0, SLOT_TILES // 2, SLOT_TILES // 2, "bank_b")
-        biased1 = biased_products(1)
-        direct_half(0, "bank_a", QUARTER)
-        direct_half(1, "bank_b", HALF)
-        turn_back(biased1, 1, 0, SLOT_TILES, "bank_c")
+        def turn_back(biased, blk):
+            back = psum.tile([P, SLOT_TILES, P], F32, name="back%d" % blk)
+            for c in range(SLOT_TILES):
+                nc.tensor.transpose(back[:, c, :], biased[:, c, :], ident[:])
+            nc.scalar.copy(score[blk][:, 0:HALF], back[:].rearrange("p c q -> p (c q)"))
+
+        def direct_product(blk, tag):
+            users = slice(blk * P, (blk + 1) * P)
+            direct = psum.tile([P, HALF], F32, name="direct%d" % blk, tag=tag)
+            for part in range(2):
+                slots = slice(part * QUARTER, (part + 1) * QUARTER)
+                nc.tensor.matmul_mx(
+                    out=direct[:, slots],
+                    lhsT=q_codes[:, users].bitcast(FP8X4),
+                    lhsT_scale=q_scales[:, users],
+                    rhs=words1[part][:].bitcast(FP4X4),
+                    rhs_scale=scales1[:, slots],
+                    start=True,
+                    stop=True,
+                )
+            return direct
+
+        biased = [
+            reused.tile([P, SLOT_TILES, P], F32, name="biased%d" % blk, align_bytes=64, offset=4096)
+            for blk in range(Q // P)
+        ]
+        biased_products(0, biased[0], 0, 2, "bank_a")
+        biased_products(0, biased[0], 2, 2, "bank_b")
+        turn_back(biased[0], 0)
+        direct0 = direct_product(0, "bank_a")
+        direct1 = direct_product(1, "bank_b")
+        for lo in (0, QUARTER):
+            nc.vector.tensor_tensor(
+                score[0][:, HALF + lo : HALF + lo + QUARTER],
+                direct0[:, lo : lo + QUARTER],
+                biases1[:, lo : lo + QUARTER],
+                ALU.add,
+            )
+        plain1 = keep.tile([P, HALF], F32, name="plain1", align_bytes=64)
+        nc.scalar.copy(plain1[:], direct1[:])
+        nc.gpsimd.tensor_tensor(score[1][:, HALF:I], plain1[:], biases1[:], ALU.add)
+        biased_products(1, biased[1], 0, SLOT_TILES, "bank_c")
+        turn_back(biased[1], 1)
 
         for blk, widths in enumerate(PAIR_PIECES):
             second = keep.tile([P, J], F32, name="second%d" % blk, align_bytes=64)
@@ -172,7 +194,9 @@ def tile_attend_pairprefs_kernel(tc, query, item_words, item_scales, ib, offs, o
                     second[:, lo:hi],
                     ALU.subtract,
                 )
-                result = keep.tile([P, width], F32, name="result%d_%d" % (blk, lo), align_bytes=64)
+                result = reused.tile(
+                    [P, width], F32, name="result%d_%d" % (blk, lo), align_bytes=64, offset=4096 + 4 * (blk * J + lo)
+                )
                 nc.scalar.activation(result[:], diff[:], ACT.Sigmoid)
                 nc.sync.dma_start(out[blk * P : (blk + 1) * P, lo:hi], result[:])
                 lo = hi

@@ -25,7 +25,7 @@ LANES = 16
 HALF = I // 2
 QUARTER = HALF // 2
 SLOT_TILES = HALF // P
-PAIR_PIECES = [(256, 256), (256, 128, 128)]
+STORE_PIECES = [((256, 256),), ((256,), (128,), (128,))]
 
 
 def tile_attend_pairprefs_kernel(tc, query, item_words, item_scales, ib, offs, offs2, offs3, out):
@@ -44,7 +44,10 @@ def tile_attend_pairprefs_kernel(tc, query, item_words, item_scales, ib, offs, o
         word_pool = keep.tile([P, T], U16, name="word_pool", align_bytes=64)
         bias_row = keep.tile([P, T], F32, name="bias_row", align_bytes=64)
         bias_pool = keep.tile([P, T], F32, name="bias_pool", align_bytes=64)
-        q_raw = reused.tile([P, PACK, Q], F32, name="q_raw", align_bytes=64, offset=0)
+        q_raw = [
+            reused.tile([P, PACK, P], F32, name="q_raw%d" % blk, align_bytes=64, offset=offset)
+            for blk, offset in enumerate((2624, 0))
+        ]
 
         nc.gpsimd.memset(scale_pool[:].bitcast(I32), 0)
         ident = keep.tile([P, P], F32, name="ident", align_bytes=64)
@@ -53,13 +56,14 @@ def tile_attend_pairprefs_kernel(tc, query, item_words, item_scales, ib, offs, o
         nc.vector.memset(bias_row[0:LAST, :].bitcast(I32), 0)
         nc.sync.dma_start(slot_list[:], offs)
         nc.sync.dma_start(bias_row[LAST:P, :], ib[LAST:P, :])
-        nc.sync.dma_start(word_pool[:].bitcast(I32), item_words[0].bitcast(I32))
         for quad in range(P // QUADRANT):
             nc.sync.dma_start(
                 scale_pool[QUADRANT * quad : QUADRANT * quad + PACK, :].bitcast(I32),
                 item_scales[0, PACK * quad : PACK * quad + PACK, :].bitcast(I32),
             )
-        nc.sync.dma_start(q_raw[:], query.rearrange("(p t) q -> p t q", t=PACK))
+        nc.sync.dma_start(word_pool[:].bitcast(I32), item_words[0].bitcast(I32))
+        for blk in range(Q // P):
+            nc.sync.dma_start(q_raw[blk][:], query[:, blk * P : (blk + 1) * P].rearrange("(p t) q -> p t q", t=PACK))
         nc.sync.dma_start(bias_pool[:], ib)
         nc.sync.dma_start(second_list[:], offs3)
         nc.sync.dma_start(first_list[:], offs2)
@@ -71,7 +75,7 @@ def tile_attend_pairprefs_kernel(tc, query, item_words, item_scales, ib, offs, o
         for blk in range(Q // P):
             nc.scalar.copy(
                 grouped[:, blk * P : (blk + 1) * P, :].rearrange("p (c i) t -> p c t i", i=PACK),
-                q_raw[:, :, blk * P : (blk + 1) * P].rearrange("p t (c i) -> p c t i", i=PACK),
+                q_raw[blk][:].rearrange("p t (c i) -> p c t i", i=PACK),
             )
 
         def quantize(blk):
@@ -94,13 +98,13 @@ def tile_attend_pairprefs_kernel(tc, query, item_words, item_scales, ib, offs, o
         ]
         scales1 = reused.tile([P, HALF], U8, name="scales1", align_bytes=64, offset=0)
         biases1 = reused.tile([P, HALF], F32, name="biases1", align_bytes=64, offset=512)
-        columns = reused.tile([P, SLOT_TILES], F32, name="columns", align_bytes=64, offset=2560)
+        columns = reused.tile([P, SLOT_TILES], F32, name="columns", align_bytes=64, offset=3136)
         q_codes = keep.tile([P, Q], U32, name="q_codes", align_bytes=64)
         q_scales = keep.tile([P, Q], U8, name="q_scales", align_bytes=64)
 
         gather(biases0[:], bias_row, 0, HALF)
-        gather(words0[:], word_pool, 0, HALF)
         gather(scales0[:], scale_pool, 0, HALF)
+        gather(words0[:], word_pool, 0, HALF)
         gather(words1[0][:], word_pool, HALF, HALF + QUARTER)
         quantize(0)
         gather(words1[1][:], word_pool, HALF + QUARTER, I)
@@ -111,7 +115,7 @@ def tile_attend_pairprefs_kernel(tc, query, item_words, item_scales, ib, offs, o
 
         score = [keep.tile([P, I], F32, name="score%d" % blk, align_bytes=64) for blk in range(Q // P)]
 
-        turned = psum.tile([P, SLOT_TILES, P], F32, name="turned")
+        turned = psum.tile([P, SLOT_TILES, P], F32, name="turned", tag="turned")
         for c in range(SLOT_TILES):
             nc.tensor.transpose(turned[:, c, :], biases0[:, c * P : (c + 1) * P], ident[:])
         nc.scalar.copy(columns[:], turned[:, :, LAST])
@@ -135,11 +139,12 @@ def tile_attend_pairprefs_kernel(tc, query, item_words, item_scales, ib, offs, o
                     biased[:, first + c, :], acc[:, c, :], ACT.Identity, bias=columns[:, first + c : first + c + 1]
                 )
 
-        def turn_back(biased, blk):
-            back = psum.tile([P, SLOT_TILES, P], F32, name="back%d" % blk)
-            for c in range(SLOT_TILES):
-                nc.tensor.transpose(back[:, c, :], biased[:, c, :], ident[:])
-            nc.scalar.copy(score[blk][:, 0:HALF], back[:].rearrange("p c q -> p (c q)"))
+        def turn_back(biased, blk, tags):
+            for first, tag in zip((0, 2), tags):
+                back = psum.tile([P, 2, P], F32, name="back%d_%d" % (blk, first), tag=tag)
+                for c in range(2):
+                    nc.tensor.transpose(back[:, c, :], biased[:, first + c, :], ident[:])
+                nc.scalar.copy(score[blk][:, first * P : (first + 2) * P], back[:].rearrange("p c q -> p (c q)"))
 
         def direct_product(blk, tag):
             users = slice(blk * P, (blk + 1) * P)
@@ -158,12 +163,12 @@ def tile_attend_pairprefs_kernel(tc, query, item_words, item_scales, ib, offs, o
             return direct
 
         biased = [
-            reused.tile([P, SLOT_TILES, P], F32, name="biased%d" % blk, align_bytes=64, offset=4096)
+            reused.tile([P, SLOT_TILES, P], F32, name="biased%d" % blk, align_bytes=64, offset=4736)
             for blk in range(Q // P)
         ]
         biased_products(0, biased[0], 0, 2, "bank_a")
         biased_products(0, biased[0], 2, 2, "bank_b")
-        turn_back(biased[0], 0)
+        turn_back(biased[0], 0, ("bank_c", "bank_d"))
         direct0 = direct_product(0, "bank_a")
         direct1 = direct_product(1, "bank_b")
         for lo in (0, QUARTER):
@@ -176,27 +181,28 @@ def tile_attend_pairprefs_kernel(tc, query, item_words, item_scales, ib, offs, o
         plain1 = keep.tile([P, HALF], F32, name="plain1", align_bytes=64)
         nc.scalar.copy(plain1[:], direct1[:])
         nc.gpsimd.tensor_tensor(score[1][:, HALF:I], plain1[:], biases1[:], ALU.add)
-        biased_products(1, biased[1], 0, SLOT_TILES, "bank_c")
-        turn_back(biased[1], 1)
+        biased_products(1, biased[1], 0, 2, "bank_c")
+        biased_products(1, biased[1], 2, 2, "bank_d")
+        turn_back(biased[1], 1, ("bank_e", "bank_f"))
 
-        for blk, widths in enumerate(PAIR_PIECES):
+        for blk, stores in enumerate(STORE_PIECES):
             second = keep.tile([P, J], F32, name="second%d" % blk, align_bytes=64)
             for lo in (0, J // 2):
                 entries = second_list[:, lo // LANES : (lo + J // 2) // LANES]
                 nc.vector.tensor_copy(second[:, lo : lo + J // 2], score[blk][:].indirect(entries))
+            result = reused.tile([P, J], F32, name="result%d" % blk, align_bytes=64, offset=4736 + 4 * J * blk)
             lo = 0
-            for width in widths:
-                hi = lo + width
-                diff = keep.tile([P, width], F32, name="diff%d_%d" % (blk, lo), align_bytes=64)
-                nc.vector.tensor_tensor(
-                    diff[:],
-                    score[blk][:].indirect(first_list[:, lo // LANES : hi // LANES]),
-                    second[:, lo:hi],
-                    ALU.subtract,
-                )
-                result = reused.tile(
-                    [P, width], F32, name="result%d_%d" % (blk, lo), align_bytes=64, offset=4096 + 4 * (blk * J + lo)
-                )
-                nc.scalar.activation(result[:], diff[:], ACT.Sigmoid)
-                nc.sync.dma_start(out[blk * P : (blk + 1) * P, lo:hi], result[:])
-                lo = hi
+            for widths in stores:
+                start = lo
+                for width in widths:
+                    hi = lo + width
+                    diff = keep.tile([P, width], F32, name="diff%d_%d" % (blk, lo), align_bytes=64)
+                    nc.vector.tensor_tensor(
+                        diff[:],
+                        score[blk][:].indirect(first_list[:, lo // LANES : hi // LANES]),
+                        second[:, lo:hi],
+                        ALU.subtract,
+                    )
+                    nc.scalar.activation(result[:, lo:hi], diff[:], ACT.Sigmoid)
+                    lo = hi
+                nc.sync.dma_start(out[blk * P : (blk + 1) * P, start:lo], result[:, start:lo])

@@ -25,7 +25,15 @@ LANES = 16
 HALF = I // 2
 QUARTER = HALF // 2
 SLOT_TILES = HALF // P
-STORE_PIECES = [((256, 256),), ((256,), (128,), (128,))]
+USER_TILES = Q // P
+PAIR_PIECES = [((256, 256),), ((256,), (128,), (128,))]
+
+AT_RAW1 = 0
+AT_BIASES1 = AT_RAW1 + QUARTER
+AT_RAW0 = AT_BIASES1 + 4 * HALF
+AT_COLUMNS = AT_RAW0 + 2 * HALF
+AT_BIASED = AT_RAW0 + 4 * PACK * P
+AT_RESULT1 = AT_BIASED + 4 * J
 
 
 def tile_attend_pairprefs_kernel(tc, query, item_words, item_scales, ib, offs, offs2, offs3, out):
@@ -45,90 +53,90 @@ def tile_attend_pairprefs_kernel(tc, query, item_words, item_scales, ib, offs, o
         bias_row = keep.tile([P, T], F32, name="bias_row", align_bytes=64)
         bias_pool = keep.tile([P, T], F32, name="bias_pool", align_bytes=64)
         q_raw = [
-            reused.tile([P, PACK, P], F32, name="q_raw%d" % blk, align_bytes=64, offset=offset)
-            for blk, offset in enumerate((2624, 0))
+            reused.tile([P, PACK, P], F32, name="q_raw%d" % ut, align_bytes=64, offset=offset)
+            for ut, offset in enumerate((AT_RAW0, AT_RAW1))
         ]
 
         nc.gpsimd.memset(scale_pool[:].bitcast(I32), 0)
         ident = keep.tile([P, P], F32, name="ident", align_bytes=64)
         make_identity(nc, ident[:])
-
         nc.vector.memset(bias_row[0:LAST, :].bitcast(I32), 0)
+
         nc.sync.dma_start(slot_list[:], offs)
         nc.sync.dma_start(bias_row[LAST:P, :], ib[LAST:P, :])
-        for quad in range(P // QUADRANT):
+        for r in range(PACK):
             nc.sync.dma_start(
-                scale_pool[QUADRANT * quad : QUADRANT * quad + PACK, :].bitcast(I32),
-                item_scales[0, PACK * quad : PACK * quad + PACK, :].bitcast(I32),
+                scale_pool[r:P:QUADRANT, :].bitcast(I32), item_scales[0, r : D // QUADRANT : PACK, :].bitcast(I32)
             )
         nc.sync.dma_start(word_pool[:].bitcast(I32), item_words[0].bitcast(I32))
-        for blk in range(Q // P):
-            nc.sync.dma_start(q_raw[blk][:], query[:, blk * P : (blk + 1) * P].rearrange("(p t) q -> p t q", t=PACK))
+        for ut in range(USER_TILES):
+            nc.sync.dma_start(q_raw[ut][:], query[:, ut * P : (ut + 1) * P].rearrange("(p t) q -> p t q", t=PACK))
         nc.sync.dma_start(bias_pool[:], ib)
         nc.sync.dma_start(second_list[:], offs3)
         nc.sync.dma_start(first_list[:], offs2)
 
         warm = keep.tile([P, 1], F32, name="warm", align_bytes=64)
-        nc.scalar.activation(warm[:], ident[:, 0:1], ACT.Sigmoid)
+        nc.scalar.activation(warm[0:QUADRANT, :], bias_row[0:QUADRANT, 0:1], ACT.Sigmoid)
 
         grouped = keep.tile([P, Q, PACK], BF16, name="grouped", align_bytes=64)
-        for blk in range(Q // P):
+        for ut in range(USER_TILES):
             nc.scalar.copy(
-                grouped[:, blk * P : (blk + 1) * P, :].rearrange("p (c i) t -> p c t i", i=PACK),
-                q_raw[blk][:].rearrange("p t (c i) -> p c t i", i=PACK),
+                grouped[:, ut * P : (ut + 1) * P, :].rearrange("p (c i) t -> p c t i", i=PACK),
+                q_raw[ut][:].rearrange("p t (c i) -> p c t i", i=PACK),
             )
 
-        def quantize(blk):
-            users = slice(blk * P, (blk + 1) * P)
+        biases0 = keep.tile([P, HALF], F32, name="biases0", align_bytes=64)
+        words0 = keep.tile([P, HALF], U16, name="words0", align_bytes=64)
+        early_scales = keep.tile([P, HALF + QUARTER], U8, name="early_scales", align_bytes=64)
+        words1 = reused.tile([P, HALF], U16, name="words1", align_bytes=64, offset=AT_RAW0)
+        last_scales = reused.tile([P, QUARTER], U8, name="last_scales", align_bytes=64, offset=AT_RAW1)
+        biases1 = reused.tile([P, HALF], F32, name="biases1", align_bytes=64, offset=AT_BIASES1)
+        columns = reused.tile([P, SLOT_TILES], F32, name="columns", align_bytes=64, offset=AT_COLUMNS)
+        q_codes = keep.tile([P, Q], U32, name="q_codes", align_bytes=64)
+        q_scales = keep.tile([P, Q], U8, name="q_scales", align_bytes=64)
+
+        def gather(got, window, lo, hi):
+            nc.vector.tensor_copy(got, window[:].indirect(slot_list[:, lo // LANES : hi // LANES]))
+
+        def quantize(ut):
+            users = slice(ut * P, (ut + 1) * P)
             nc.vector.quantize_mx(
                 out=q_codes[:, users].bitcast(FP8X4),
                 scales=q_scales[:, users],
                 in_=grouped[:, users, :].rearrange("p q t -> p (q t)"),
             )
 
-        def gather(got, window, lo, hi):
-            nc.vector.tensor_copy(got, window[:].indirect(slot_list[:, lo // LANES : hi // LANES]))
-
-        biases0 = keep.tile([P, HALF], F32, name="biases0", align_bytes=64)
-        words0 = keep.tile([P, HALF], U16, name="words0", align_bytes=64)
-        scales0 = keep.tile([P, HALF], U8, name="scales0", align_bytes=64)
-        words1 = [
-            keep.tile([P, QUARTER], U16, name="words1a", align_bytes=64),
-            reused.tile([P, QUARTER], U16, name="words1b", align_bytes=64, offset=2624),
-        ]
-        scales1 = reused.tile([P, HALF], U8, name="scales1", align_bytes=64, offset=0)
-        biases1 = reused.tile([P, HALF], F32, name="biases1", align_bytes=64, offset=512)
-        columns = reused.tile([P, SLOT_TILES], F32, name="columns", align_bytes=64, offset=3136)
-        q_codes = keep.tile([P, Q], U32, name="q_codes", align_bytes=64)
-        q_scales = keep.tile([P, Q], U8, name="q_scales", align_bytes=64)
-
         gather(biases0[:], bias_row, 0, HALF)
-        gather(scales0[:], scale_pool, 0, HALF)
+        gather(early_scales[:], scale_pool, 0, HALF + QUARTER)
         gather(words0[:], word_pool, 0, HALF)
-        gather(words1[0][:], word_pool, HALF, HALF + QUARTER)
         quantize(0)
-        gather(words1[1][:], word_pool, HALF + QUARTER, I)
+        gather(words1[:], word_pool, HALF, I)
         quantize(1)
-        gather(scales1[:], scale_pool, HALF, I)
+        gather(last_scales[:], scale_pool, HALF + QUARTER, I)
         for lo in (0, QUARTER):
             gather(biases1[:, lo : lo + QUARTER], bias_pool, HALF + lo, HALF + lo + QUARTER)
 
-        score = [keep.tile([P, I], F32, name="score%d" % blk, align_bytes=64) for blk in range(Q // P)]
+        score = [keep.tile([P, I], F32, name="score%d" % ut, align_bytes=64) for ut in range(USER_TILES)]
 
-        turned = psum.tile([P, SLOT_TILES, P], F32, name="turned", tag="turned")
+        turned = psum.tile([P, SLOT_TILES, P], F32, name="turned")
         for c in range(SLOT_TILES):
             nc.tensor.transpose(turned[:, c, :], biases0[:, c * P : (c + 1) * P], ident[:])
         nc.scalar.copy(columns[:], turned[:, :, LAST])
 
-        def biased_products(blk, biased, first, count, tag):
-            users = slice(blk * P, (blk + 1) * P)
-            acc = psum.tile([P, count, P], F32, name="acc%d_%d" % (blk, first), tag=tag)
+        biased = [
+            reused.tile([P, SLOT_TILES, P], F32, name="biased%d" % ut, align_bytes=64, offset=AT_BIASED)
+            for ut in range(USER_TILES)
+        ]
+
+        def biased_products(ut, first, count, bank):
+            users = slice(ut * P, (ut + 1) * P)
+            acc = psum.tile([P, count, P], F32, name="acc%d_%d" % (ut, first), tag=bank)
             for c in range(count):
                 slots = slice((first + c) * P, (first + c + 1) * P)
                 nc.tensor.matmul_mx(
                     out=acc[:, c, :],
                     lhsT=words0[:, slots].bitcast(FP4X4),
-                    lhsT_scale=scales0[:, slots],
+                    lhsT_scale=early_scales[:, slots],
                     rhs=q_codes[:, users].bitcast(FP8X4),
                     rhs_scale=q_scales[:, users],
                     start=True,
@@ -136,73 +144,72 @@ def tile_attend_pairprefs_kernel(tc, query, item_words, item_scales, ib, offs, o
                 )
             for c in range(count):
                 nc.scalar.activation(
-                    biased[:, first + c, :], acc[:, c, :], ACT.Identity, bias=columns[:, first + c : first + c + 1]
+                    biased[ut][:, first + c, :], acc[:, c, :], ACT.Identity, bias=columns[:, first + c : first + c + 1]
                 )
 
-        def turn_back(biased, blk, tags):
-            for first, tag in zip((0, 2), tags):
-                back = psum.tile([P, 2, P], F32, name="back%d_%d" % (blk, first), tag=tag)
-                for c in range(2):
-                    nc.tensor.transpose(back[:, c, :], biased[:, first + c, :], ident[:])
-                nc.scalar.copy(score[blk][:, first * P : (first + 2) * P], back[:].rearrange("p c q -> p (c q)"))
+        def turn_back(ut, banks):
+            share = SLOT_TILES // len(banks)
+            for k, bank in enumerate(banks):
+                first = k * share
+                back = psum.tile([P, share, P], F32, name="back%d_%d" % (ut, first), tag=bank)
+                for c in range(share):
+                    nc.tensor.transpose(back[:, c, :], biased[ut][:, first + c, :], ident[:])
+                nc.scalar.copy(score[ut][:, first * P : (first + share) * P], back[:].rearrange("p c q -> p (c q)"))
 
-        def direct_product(blk, tag):
-            users = slice(blk * P, (blk + 1) * P)
-            direct = psum.tile([P, HALF], F32, name="direct%d" % blk, tag=tag)
-            for part in range(2):
-                slots = slice(part * QUARTER, (part + 1) * QUARTER)
-                nc.tensor.matmul_mx(
-                    out=direct[:, slots],
-                    lhsT=q_codes[:, users].bitcast(FP8X4),
-                    lhsT_scale=q_scales[:, users],
-                    rhs=words1[part][:].bitcast(FP4X4),
-                    rhs_scale=scales1[:, slots],
-                    start=True,
-                    stop=True,
-                )
-            return direct
-
-        biased = [
-            reused.tile([P, SLOT_TILES, P], F32, name="biased%d" % blk, align_bytes=64, offset=4736)
-            for blk in range(Q // P)
-        ]
-        biased_products(0, biased[0], 0, 2, "bank_a")
-        biased_products(0, biased[0], 2, 2, "bank_b")
-        turn_back(biased[0], 0, ("bank_c", "bank_d"))
-        direct0 = direct_product(0, "bank_a")
-        direct1 = direct_product(1, "bank_b")
-        for lo in (0, QUARTER):
-            nc.vector.tensor_tensor(
-                score[0][:, HALF + lo : HALF + lo + QUARTER],
-                direct0[:, lo : lo + QUARTER],
-                biases1[:, lo : lo + QUARTER],
-                ALU.add,
+        def direct_product(direct, ut, part):
+            users = slice(ut * P, (ut + 1) * P)
+            nc.tensor.matmul_mx(
+                out=direct,
+                lhsT=q_codes[:, users].bitcast(FP8X4),
+                lhsT_scale=q_scales[:, users],
+                rhs=words1[:, part * QUARTER : (part + 1) * QUARTER].bitcast(FP4X4),
+                rhs_scale=(early_scales[:, HALF:], last_scales[:])[part],
+                start=True,
+                stop=True,
             )
-        plain1 = keep.tile([P, HALF], F32, name="plain1", align_bytes=64)
-        nc.scalar.copy(plain1[:], direct1[:])
-        nc.gpsimd.tensor_tensor(score[1][:, HALF:I], plain1[:], biases1[:], ALU.add)
-        biased_products(1, biased[1], 0, 2, "bank_c")
-        biased_products(1, biased[1], 2, 2, "bank_d")
-        turn_back(biased[1], 1, ("bank_e", "bank_f"))
 
-        for blk, stores in enumerate(STORE_PIECES):
-            second = keep.tile([P, J], F32, name="second%d" % blk, align_bytes=64)
+        biased_products(0, 0, 1, "bank_a")
+        biased_products(0, 1, 1, "bank_b")
+        biased_products(0, 2, 2, "bank_c")
+        turn_back(0, ("bank_d", "bank_e"))
+        for part, bank in enumerate(("bank_b", "bank_c")):
+            direct0 = psum.tile([P, QUARTER], F32, name="direct0_%d" % part, tag=bank)
+            direct_product(direct0[:], 0, part)
+            lo = part * QUARTER
+            nc.vector.tensor_tensor(
+                score[0][:, HALF + lo : HALF + lo + QUARTER], direct0[:], biases1[:, lo : lo + QUARTER], ALU.add
+            )
+
+        direct1 = psum.tile([P, HALF], F32, name="direct1", tag="bank_d")
+        for part in range(HALF // QUARTER):
+            direct_product(direct1[:, part * QUARTER : (part + 1) * QUARTER], 1, part)
+        unbiased1 = keep.tile([P, HALF], F32, name="unbiased1", align_bytes=64)
+        nc.scalar.copy(unbiased1[:], direct1[:])
+        nc.gpsimd.tensor_tensor(score[1][:, HALF:I], unbiased1[:], biases1[:], ALU.add)
+        biased_products(1, 0, 2, "bank_e")
+        biased_products(1, 2, 2, "bank_b")
+        turn_back(1, ("bank_f", "bank_g"))
+
+        for ut, stores in enumerate(PAIR_PIECES):
+            second = keep.tile([P, J], F32, name="second%d" % ut, align_bytes=64)
             for lo in (0, J // 2):
                 entries = second_list[:, lo // LANES : (lo + J // 2) // LANES]
-                nc.vector.tensor_copy(second[:, lo : lo + J // 2], score[blk][:].indirect(entries))
-            result = reused.tile([P, J], F32, name="result%d" % blk, align_bytes=64, offset=4736 + 4 * J * blk)
+                nc.vector.tensor_copy(second[:, lo : lo + J // 2], score[ut][:].indirect(entries))
+            result = reused.tile(
+                [P, J], F32, name="result%d" % ut, align_bytes=64, offset=(AT_BIASED, AT_RESULT1)[ut]
+            )
             lo = 0
             for widths in stores:
-                start = lo
+                stored = lo
                 for width in widths:
                     hi = lo + width
-                    diff = keep.tile([P, width], F32, name="diff%d_%d" % (blk, lo), align_bytes=64)
+                    diff = keep.tile([P, width], F32, name="diff%d_%d" % (ut, lo), align_bytes=64)
                     nc.vector.tensor_tensor(
                         diff[:],
-                        score[blk][:].indirect(first_list[:, lo // LANES : hi // LANES]),
+                        score[ut][:].indirect(first_list[:, lo // LANES : hi // LANES]),
                         second[:, lo:hi],
                         ALU.subtract,
                     )
                     nc.scalar.activation(result[:, lo:hi], diff[:], ACT.Sigmoid)
                     lo = hi
-                nc.sync.dma_start(out[blk * P : (blk + 1) * P, start:lo], result[:, start:lo])
+                nc.sync.dma_start(out[ut * P : (ut + 1) * P, stored:lo], result[:, stored:lo])

@@ -75,9 +75,6 @@ def tile_attend_pairprefs_kernel(tc, query, item_words, item_scales, ib, offs, o
         nc.sync.dma_start(second_list[:], offs3)
         nc.sync.dma_start(first_list[:], offs2)
 
-        warm = keep.tile([P, 1], F32, name="warm", align_bytes=64)
-        nc.scalar.activation(warm[0:QUADRANT, :], bias_row[0:QUADRANT, 0:1], ACT.Sigmoid)
-
         grouped = keep.tile([P, Q, PACK], BF16, name="grouped", align_bytes=64)
         for ut in range(USER_TILES):
             nc.scalar.copy(

@@ -57,13 +57,14 @@ def tile_attend_pairprefs_kernel(tc, query, item_words, item_scales, ib, offs, o
             for ut, offset in enumerate((AT_RAW0, AT_RAW1))
         ]
 
-        nc.gpsimd.memset(scale_pool[:].bitcast(I32), 0)
-        ident = keep.tile([P, P], F32, name="ident", align_bytes=64)
-        make_identity(nc, ident[:])
+        nc.vector.memset(scale_pool[:].bitcast(I32), 0)
         nc.vector.memset(bias_row[0:LAST, :].bitcast(I32), 0)
+        ident = keep.tile([P, P], F32, name="ident", align_bytes=64)
+        nc.vector.memset(ident[:], 0.0)
+        make_identity(nc, ident[:], nomemset=True)
 
-        nc.sync.dma_start(slot_list[:], offs)
         nc.sync.dma_start(bias_row[LAST:P, :], ib[LAST:P, :])
+        nc.sync.dma_start(slot_list[:], offs)
         for r in range(PACK):
             nc.sync.dma_start(
                 scale_pool[r:P:QUADRANT, :].bitcast(I32), item_scales[0, r : D // QUADRANT : PACK, :].bitcast(I32)

@@ -26,7 +26,7 @@ HALF = I // 2
 QUARTER = HALF // 2
 SLOT_TILES = HALF // P
 USER_TILES = Q // P
-PAIR_PIECES = [((256, 256),), ((256,), (128,), (128,))]
+PAIR_PIECES = [((256, 256),), ((256,), (128,), (64, 64))]
 
 AT_RAW1 = 0
 AT_BIASES1 = AT_RAW1 + QUARTER
@@ -170,20 +170,20 @@ def tile_attend_pairprefs_kernel(tc, query, item_words, item_scales, ib, offs, o
         biased_products(0, 1, 1, "bank_b")
         biased_products(0, 2, 2, "bank_c")
         turn_back(0, ("bank_d", "bank_e"))
-        for part, bank in enumerate(("bank_b", "bank_c")):
-            direct0 = psum.tile([P, QUARTER], F32, name="direct0_%d" % part, tag=bank)
-            direct_product(direct0[:], 0, part)
-            lo = part * QUARTER
-            nc.vector.tensor_tensor(
-                score[0][:, HALF + lo : HALF + lo + QUARTER], direct0[:], biases1[:, lo : lo + QUARTER], ALU.add
-            )
+        third0 = psum.tile([P, QUARTER], F32, name="third0", tag="bank_b")
+        direct_product(third0[:], 0, 0)
+        last = psum.tile([P, USER_TILES, QUARTER], F32, name="last", tag="bank_c")
+        for ut in range(USER_TILES):
+            direct_product(last[:, ut, :], ut, 1)
+        nc.vector.tensor_tensor(score[0][:, HALF : HALF + QUARTER], third0[:], biases1[:, 0:QUARTER], ALU.add)
+        for ut in range(USER_TILES):
+            nc.vector.tensor_tensor(score[ut][:, HALF + QUARTER : I], last[:, ut, :], biases1[:, QUARTER:HALF], ALU.add)
 
-        direct1 = psum.tile([P, HALF], F32, name="direct1", tag="bank_d")
-        for part in range(HALF // QUARTER):
-            direct_product(direct1[:, part * QUARTER : (part + 1) * QUARTER], 1, part)
-        unbiased1 = keep.tile([P, HALF], F32, name="unbiased1", align_bytes=64)
-        nc.scalar.copy(unbiased1[:], direct1[:])
-        nc.gpsimd.tensor_tensor(score[1][:, HALF:I], unbiased1[:], biases1[:], ALU.add)
+        third1 = psum.tile([P, QUARTER], F32, name="third1", tag="bank_d")
+        direct_product(third1[:], 1, 0)
+        unbiased1 = keep.tile([P, QUARTER], F32, name="unbiased1", align_bytes=64)
+        nc.scalar.copy(unbiased1[:], third1[:])
+        nc.gpsimd.tensor_tensor(score[1][:, HALF : HALF + QUARTER], unbiased1[:], biases1[:, 0:QUARTER], ALU.add)
         biased_products(1, 0, 2, "bank_e")
         biased_products(1, 2, 2, "bank_b")
         turn_back(1, ("bank_f", "bank_g"))

@@ -29,9 +29,10 @@ USER_TILES = Q // P
 PAIR_PIECES = [((256, 256),), ((256,), (128,), (64, 64))]
 
 AT_RAW1 = 0
-AT_BIASES1 = AT_RAW1 + QUARTER
+AT_BIASES1 = AT_RAW1
 AT_RAW0 = AT_BIASES1 + 4 * HALF
-AT_COLUMNS = AT_RAW0 + 2 * HALF
+AT_WORDS2 = AT_RAW0 + 2 * QUARTER
+AT_COLUMNS = AT_WORDS2 + 2 * HALF
 AT_BIASED = AT_RAW0 + 4 * PACK * P
 AT_RESULT1 = AT_BIASED + 4 * J
 
@@ -69,9 +70,9 @@ def tile_attend_pairprefs_kernel(tc, query, item_words, item_scales, ib, offs, o
             nc.sync.dma_start(
                 scale_pool[r:P:QUADRANT, :].bitcast(I32), item_scales[0, r : D // QUADRANT : PACK, :].bitcast(I32)
             )
+        nc.sync.dma_start(q_raw[0][:], query[:, 0:P].rearrange("(p t) q -> p t q", t=PACK))
         nc.sync.dma_start(word_pool[:].bitcast(I32), item_words[0].bitcast(I32))
-        for ut in range(USER_TILES):
-            nc.sync.dma_start(q_raw[ut][:], query[:, ut * P : (ut + 1) * P].rearrange("(p t) q -> p t q", t=PACK))
+        nc.sync.dma_start(q_raw[1][:], query[:, P:Q].rearrange("(p t) q -> p t q", t=PACK))
         nc.sync.dma_start(bias_pool[:], ib)
         nc.sync.dma_start(second_list[:], offs3)
         nc.sync.dma_start(first_list[:], offs2)
@@ -84,10 +85,12 @@ def tile_attend_pairprefs_kernel(tc, query, item_words, item_scales, ib, offs, o
             )
 
         biases0 = keep.tile([P, HALF], F32, name="biases0", align_bytes=64)
-        words0 = keep.tile([P, HALF], U16, name="words0", align_bytes=64)
-        early_scales = keep.tile([P, HALF + QUARTER], U8, name="early_scales", align_bytes=64)
-        words1 = reused.tile([P, HALF], U16, name="words1", align_bytes=64, offset=AT_RAW0)
-        last_scales = reused.tile([P, QUARTER], U8, name="last_scales", align_bytes=64, offset=AT_RAW1)
+        early_scales = keep.tile([P, I], U8, name="early_scales", align_bytes=64)
+        words0 = [
+            keep.tile([P, QUARTER], U16, name="words0a", align_bytes=64),
+            reused.tile([P, QUARTER], U16, name="words0b", align_bytes=64, offset=AT_RAW0),
+        ]
+        words1 = reused.tile([P, HALF], U16, name="words1", align_bytes=64, offset=AT_WORDS2)
         biases1 = reused.tile([P, HALF], F32, name="biases1", align_bytes=64, offset=AT_BIASES1)
         columns = reused.tile([P, SLOT_TILES], F32, name="columns", align_bytes=64, offset=AT_COLUMNS)
         q_codes = keep.tile([P, Q], U32, name="q_codes", align_bytes=64)
@@ -105,18 +108,18 @@ def tile_attend_pairprefs_kernel(tc, query, item_words, item_scales, ib, offs, o
             )
 
         gather(biases0[:], bias_row, 0, HALF)
-        gather(early_scales[:], scale_pool, 0, HALF + QUARTER)
-        gather(words0[:], word_pool, 0, HALF)
+        gather(early_scales[:], scale_pool, 0, I)
         quantize(0)
+        gather(words0[0][:], word_pool, 0, QUARTER)
+        gather(words0[1][:], word_pool, QUARTER, HALF)
         gather(words1[:], word_pool, HALF, I)
         quantize(1)
-        gather(last_scales[:], scale_pool, HALF + QUARTER, I)
         for lo in (0, QUARTER):
             gather(biases1[:, lo : lo + QUARTER], bias_pool, HALF + lo, HALF + lo + QUARTER)
 
         score = [keep.tile([P, I], F32, name="score%d" % ut, align_bytes=64) for ut in range(USER_TILES)]
 
-        turned = psum.tile([P, SLOT_TILES, P], F32, name="turned")
+        turned = psum.tile([P, SLOT_TILES, P], F32, name="turned", tag="bank_f")
         for c in range(SLOT_TILES):
             nc.tensor.transpose(turned[:, c, :], biases0[:, c * P : (c + 1) * P], ident[:])
         nc.scalar.copy(columns[:], turned[:, :, LAST])
@@ -133,7 +136,7 @@ def tile_attend_pairprefs_kernel(tc, query, item_words, item_scales, ib, offs, o
                 slots = slice((first + c) * P, (first + c + 1) * P)
                 nc.tensor.matmul_mx(
                     out=acc[:, c, :],
-                    lhsT=words0[:, slots].bitcast(FP4X4),
+                    lhsT=words0[(first + c) // 2][:, (first + c) % 2 * P : ((first + c) % 2 + 1) * P].bitcast(FP4X4),
                     lhsT_scale=early_scales[:, slots],
                     rhs=q_codes[:, users].bitcast(FP8X4),
                     rhs_scale=q_scales[:, users],
@@ -161,14 +164,15 @@ def tile_attend_pairprefs_kernel(tc, query, item_words, item_scales, ib, offs, o
                 lhsT=q_codes[:, users].bitcast(FP8X4),
                 lhsT_scale=q_scales[:, users],
                 rhs=words1[:, part * QUARTER : (part + 1) * QUARTER].bitcast(FP4X4),
-                rhs_scale=(early_scales[:, HALF:], last_scales[:])[part],
+                rhs_scale=early_scales[:, HALF + part * QUARTER : HALF + (part + 1) * QUARTER],
                 start=True,
                 stop=True,
             )
 
         biased_products(0, 0, 1, "bank_a")
         biased_products(0, 1, 1, "bank_b")
-        biased_products(0, 2, 2, "bank_c")
+        biased_products(0, 2, 1, "bank_h")
+        biased_products(0, 3, 1, "bank_c")
         turn_back(0, ("bank_d", "bank_e"))
         third0 = psum.tile([P, QUARTER], F32, name="third0", tag="bank_b")
         direct_product(third0[:], 0, 0)

@@ -23,18 +23,13 @@ QUADRANT = 32
 LAST = P - 1
 LANES = 16
 HALF = I // 2
-QUARTER = HALF // 2
 SLOT_TILES = HALF // P
 USER_TILES = Q // P
 PAIR_PIECES = [((256, 256),), ((256,), (128,), (64, 64))]
 
-AT_RAW1 = 0
-AT_BIASES1 = AT_RAW1
-AT_RAW0 = AT_BIASES1 + 4 * HALF
-AT_WORDS2 = AT_RAW0 + 2 * QUARTER
-AT_COLUMNS = AT_WORDS2 + 2 * HALF
-AT_BIASED = AT_RAW0 + 4 * PACK * P
-AT_RESULT1 = AT_BIASED + 4 * J
+AT_WORDS1 = 0
+AT_RAW = 2 * HALF - 64
+AT_SPREAD = 2 * HALF
 
 
 def tile_attend_pairprefs_kernel(tc, query, item_words, item_scales, ib, offs, offs2, offs3, out):
@@ -52,11 +47,7 @@ def tile_attend_pairprefs_kernel(tc, query, item_words, item_scales, ib, offs, o
         scale_pool = keep.tile([P, T], U8, name="scale_pool", align_bytes=64)
         word_pool = keep.tile([P, T], U16, name="word_pool", align_bytes=64)
         bias_row = keep.tile([P, T], F32, name="bias_row", align_bytes=64)
-        bias_pool = keep.tile([P, T], F32, name="bias_pool", align_bytes=64)
-        q_raw = [
-            reused.tile([P, PACK, P], F32, name="q_raw%d" % ut, align_bytes=64, offset=offset)
-            for ut, offset in enumerate((AT_RAW0, AT_RAW1))
-        ]
+        q_raw = reused.tile([P, PACK, Q], F32, name="q_raw", align_bytes=64, offset=AT_RAW)
 
         nc.vector.memset(scale_pool[:].bitcast(I32), 0)
         nc.vector.memset(bias_row[0:LAST, :].bitcast(I32), 0)
@@ -70,136 +61,85 @@ def tile_attend_pairprefs_kernel(tc, query, item_words, item_scales, ib, offs, o
             nc.sync.dma_start(
                 scale_pool[r:P:QUADRANT, :].bitcast(I32), item_scales[0, r : D // QUADRANT : PACK, :].bitcast(I32)
             )
-        nc.sync.dma_start(q_raw[0][:], query[:, 0:P].rearrange("(p t) q -> p t q", t=PACK))
         nc.sync.dma_start(word_pool[:].bitcast(I32), item_words[0].bitcast(I32))
-        nc.sync.dma_start(q_raw[1][:], query[:, P:Q].rearrange("(p t) q -> p t q", t=PACK))
-        nc.sync.dma_start(bias_pool[:], ib)
+        nc.sync.dma_start(q_raw[:], query.rearrange("(p t) q -> p t q", t=PACK))
         nc.sync.dma_start(second_list[:], offs3)
         nc.sync.dma_start(first_list[:], offs2)
 
-        grouped = keep.tile([P, Q, PACK], BF16, name="grouped", align_bytes=64)
-        for ut in range(USER_TILES):
-            nc.scalar.copy(
-                grouped[:, ut * P : (ut + 1) * P, :].rearrange("p (c i) t -> p c t i", i=PACK),
-                q_raw[ut][:].rearrange("p t (c i) -> p c t i", i=PACK),
-            )
+        def entries(tile, lo, hi):
+            return tile[:, lo // LANES : hi // LANES]
 
-        biases0 = keep.tile([P, HALF], F32, name="biases0", align_bytes=64)
-        early_scales = keep.tile([P, I], U8, name="early_scales", align_bytes=64)
-        words0 = [
-            keep.tile([P, QUARTER], U16, name="words0a", align_bytes=64),
-            reused.tile([P, QUARTER], U16, name="words0b", align_bytes=64, offset=AT_RAW0),
+        columns = keep.tile([P, I // P], F32, name="columns", align_bytes=64)
+        biases = [keep.tile([P, HALF], F32, name="biases%d" % h, align_bytes=64) for h in range(2)]
+        for h in range(2):
+            nc.scalar.activation(biases[h][:], bias_row[:].indirect(entries(slot_list, h * HALF, (h + 1) * HALF)), ACT.Copy)
+        spread_banks = []
+        for h in range(2):
+            turned = psum.tile([P, SLOT_TILES, P], F32, name="turned%d" % h, tag="turned%d" % h)
+            for c in range(SLOT_TILES):
+                nc.tensor.transpose(turned[:, c, :], biases[h][:, c * P : (c + 1) * P], ident[:])
+            nc.scalar.copy(columns[:, h * SLOT_TILES : (h + 1) * SLOT_TILES], turned[:, :, LAST])
+            bank = psum.tile([P, SLOT_TILES, P], F32, name="spread_bank%d" % h, tag="spread%d" % h)
+            for c in range(SLOT_TILES):
+                k = h * SLOT_TILES + c
+                nc.tensor.transpose(bank[:, c, :], columns[:, k : k + 1].to_broadcast([P, P]), ident[:])
+            spread_banks.append(bank)
+
+        grouped = keep.tile([P, Q, PACK], BF16, name="grouped", align_bytes=64)
+        nc.scalar.copy(
+            grouped[:].rearrange("p (c i) t -> p c t i", i=PACK),
+            q_raw[:].rearrange("p t (c i) -> p c t i", i=PACK),
+        )
+        spread = [
+            reused.tile([P, HALF], F32, name="spread%d" % h, align_bytes=64, offset=AT_SPREAD + 4 * HALF * h)
+            for h in range(2)
         ]
-        words1 = reused.tile([P, HALF], U16, name="words1", align_bytes=64, offset=AT_WORDS2)
-        biases1 = reused.tile([P, HALF], F32, name="biases1", align_bytes=64, offset=AT_BIASES1)
-        columns = reused.tile([P, SLOT_TILES], F32, name="columns", align_bytes=64, offset=AT_COLUMNS)
+        for h in range(2):
+            nc.scalar.copy(spread[h][:], spread_banks[h][:].rearrange("p c q -> p (c q)"))
+
+        scales = keep.tile([P, I], U8, name="scales", align_bytes=64)
+        words = [
+            keep.tile([P, HALF], U16, name="words0", align_bytes=64),
+            reused.tile([P, HALF], U16, name="words1", align_bytes=64, offset=AT_WORDS1),
+        ]
         q_codes = keep.tile([P, Q], U32, name="q_codes", align_bytes=64)
         q_scales = keep.tile([P, Q], U8, name="q_scales", align_bytes=64)
 
-        def gather(got, window, lo, hi):
-            nc.vector.tensor_copy(got, window[:].indirect(slot_list[:, lo // LANES : hi // LANES]))
-
-        def quantize(ut):
-            users = slice(ut * P, (ut + 1) * P)
-            nc.vector.quantize_mx(
-                out=q_codes[:, users].bitcast(FP8X4),
-                scales=q_scales[:, users],
-                in_=grouped[:, users, :].rearrange("p q t -> p (q t)"),
-            )
-
-        gather(biases0[:], bias_row, 0, HALF)
-        gather(early_scales[:], scale_pool, 0, I)
-        quantize(0)
-        gather(words0[0][:], word_pool, 0, QUARTER)
-        gather(words0[1][:], word_pool, QUARTER, HALF)
-        gather(words1[:], word_pool, HALF, I)
-        quantize(1)
-        for lo in (0, QUARTER):
-            gather(biases1[:, lo : lo + QUARTER], bias_pool, HALF + lo, HALF + lo + QUARTER)
+        nc.vector.tensor_copy(scales[:], scale_pool[:].indirect(slot_list[:]))
+        nc.vector.tensor_copy(words[0][:], word_pool[:].indirect(entries(slot_list, 0, HALF)))
+        nc.vector.quantize_mx(
+            out=q_codes[:].bitcast(FP8X4), scales=q_scales[:], in_=grouped[:].rearrange("p q t -> p (q t)")
+        )
+        nc.vector.tensor_copy(words[1][:], word_pool[:].indirect(entries(slot_list, HALF, I)))
 
         score = [keep.tile([P, I], F32, name="score%d" % ut, align_bytes=64) for ut in range(USER_TILES)]
-
-        turned = psum.tile([P, SLOT_TILES, P], F32, name="turned", tag="bank_f")
-        for c in range(SLOT_TILES):
-            nc.tensor.transpose(turned[:, c, :], biases0[:, c * P : (c + 1) * P], ident[:])
-        nc.scalar.copy(columns[:], turned[:, :, LAST])
-
-        biased = [
-            reused.tile([P, SLOT_TILES, P], F32, name="biased%d" % ut, align_bytes=64, offset=AT_BIASED)
-            for ut in range(USER_TILES)
-        ]
-
-        def biased_products(ut, first, count, bank):
-            users = slice(ut * P, (ut + 1) * P)
-            acc = psum.tile([P, count, P], F32, name="acc%d_%d" % (ut, first), tag=bank)
-            for c in range(count):
-                slots = slice((first + c) * P, (first + c + 1) * P)
+        products = {}
+        for h in range(2):
+            for ut in range(USER_TILES):
+                users = slice(ut * P, (ut + 1) * P)
+                acc = psum.tile([P, HALF], F32, name="acc%d_%d" % (ut, h), tag="acc%d_%d" % (ut, h))
                 nc.tensor.matmul_mx(
-                    out=acc[:, c, :],
-                    lhsT=words0[(first + c) // 2][:, (first + c) % 2 * P : ((first + c) % 2 + 1) * P].bitcast(FP4X4),
-                    lhsT_scale=early_scales[:, slots],
-                    rhs=q_codes[:, users].bitcast(FP8X4),
-                    rhs_scale=q_scales[:, users],
+                    out=acc[:],
+                    lhsT=q_codes[:, users].bitcast(FP8X4),
+                    lhsT_scale=q_scales[:, users],
+                    rhs=words[h][:].bitcast(FP4X4),
+                    rhs_scale=scales[:, h * HALF : (h + 1) * HALF],
                     start=True,
                     stop=True,
                 )
-            for c in range(count):
-                nc.scalar.activation(
-                    biased[ut][:, first + c, :], acc[:, c, :], ACT.Identity, bias=columns[:, first + c : first + c + 1]
-                )
-
-        def turn_back(ut, banks):
-            share = SLOT_TILES // len(banks)
-            for k, bank in enumerate(banks):
-                first = k * share
-                back = psum.tile([P, share, P], F32, name="back%d_%d" % (ut, first), tag=bank)
-                for c in range(share):
-                    nc.tensor.transpose(back[:, c, :], biased[ut][:, first + c, :], ident[:])
-                nc.scalar.copy(score[ut][:, first * P : (first + share) * P], back[:].rearrange("p c q -> p (c q)"))
-
-        def direct_product(direct, ut, part):
-            users = slice(ut * P, (ut + 1) * P)
-            nc.tensor.matmul_mx(
-                out=direct,
-                lhsT=q_codes[:, users].bitcast(FP8X4),
-                lhsT_scale=q_scales[:, users],
-                rhs=words1[:, part * QUARTER : (part + 1) * QUARTER].bitcast(FP4X4),
-                rhs_scale=early_scales[:, HALF + part * QUARTER : HALF + (part + 1) * QUARTER],
-                start=True,
-                stop=True,
-            )
-
-        biased_products(0, 0, 1, "bank_a")
-        biased_products(0, 1, 1, "bank_b")
-        biased_products(0, 2, 1, "bank_h")
-        biased_products(0, 3, 1, "bank_c")
-        turn_back(0, ("bank_d", "bank_e"))
-        third0 = psum.tile([P, QUARTER], F32, name="third0", tag="bank_b")
-        direct_product(third0[:], 0, 0)
-        last = psum.tile([P, USER_TILES, QUARTER], F32, name="last", tag="bank_c")
+                products[ut, h] = acc
         for ut in range(USER_TILES):
-            direct_product(last[:, ut, :], ut, 1)
-        nc.vector.tensor_tensor(score[0][:, HALF : HALF + QUARTER], third0[:], biases1[:, 0:QUARTER], ALU.add)
+            for h in range(2):
+                nc.vector.tensor_tensor(score[ut][:, h * HALF : (h + 1) * HALF], products[ut, h][:], spread[h][:], ALU.add)
+
+        second = [keep.tile([P, J], F32, name="second%d" % ut, align_bytes=64) for ut in range(USER_TILES)]
         for ut in range(USER_TILES):
-            nc.vector.tensor_tensor(score[ut][:, HALF + QUARTER : I], last[:, ut, :], biases1[:, QUARTER:HALF], ALU.add)
-
-        third1 = psum.tile([P, QUARTER], F32, name="third1", tag="bank_d")
-        direct_product(third1[:], 1, 0)
-        unbiased1 = keep.tile([P, QUARTER], F32, name="unbiased1", align_bytes=64)
-        nc.scalar.copy(unbiased1[:], third1[:])
-        nc.gpsimd.tensor_tensor(score[1][:, HALF : HALF + QUARTER], unbiased1[:], biases1[:, 0:QUARTER], ALU.add)
-        biased_products(1, 0, 2, "bank_e")
-        biased_products(1, 2, 2, "bank_b")
-        turn_back(1, ("bank_f", "bank_g"))
-
-        for ut, stores in enumerate(PAIR_PIECES):
-            second = keep.tile([P, J], F32, name="second%d" % ut, align_bytes=64)
             for lo in (0, J // 2):
-                entries = second_list[:, lo // LANES : (lo + J // 2) // LANES]
-                nc.vector.tensor_copy(second[:, lo : lo + J // 2], score[ut][:].indirect(entries))
-            result = reused.tile(
-                [P, J], F32, name="result%d" % ut, align_bytes=64, offset=(AT_BIASED, AT_RESULT1)[ut]
-            )
+                nc.scalar.activation(
+                    second[ut][:, lo : lo + J // 2], score[ut][:].indirect(entries(second_list, lo, lo + J // 2)), ACT.Copy
+                )
+        for ut, stores in enumerate(PAIR_PIECES):
+            result = keep.tile([P, J], F32, name="result%d" % ut, align_bytes=64)
             lo = 0
             for widths in stores:
                 stored = lo
@@ -207,10 +147,7 @@ def tile_attend_pairprefs_kernel(tc, query, item_words, item_scales, ib, offs, o
                     hi = lo + width
                     diff = keep.tile([P, width], F32, name="diff%d_%d" % (ut, lo), align_bytes=64)
                     nc.vector.tensor_tensor(
-                        diff[:],
-                        score[ut][:].indirect(first_list[:, lo // LANES : hi // LANES]),
-                        second[:, lo:hi],
-                        ALU.subtract,
+                        diff[:], score[ut][:].indirect(entries(first_list, lo, hi)), second[ut][:, lo:hi], ALU.subtract
                     )
                     nc.scalar.activation(result[:, lo:hi], diff[:], ACT.Sigmoid)
                     lo = hi

@@ -49,6 +49,10 @@ def tile_attend_pairprefs_kernel(tc, query, item_words, item_scales, ib, offs, o
         bias_row = keep.tile([P, T], F32, name="bias_row", align_bytes=64)
         q_raw = reused.tile([P, PACK, Q], F32, name="q_raw", align_bytes=64, offset=AT_RAW)
 
+        warm = keep.tile([P, 2], F32, name="warm", align_bytes=64)
+        nc.gpsimd.memset(warm[:, 0:1], 0.0)
+        nc.scalar.activation(warm[:, 1:2], warm[:, 0:1], ACT.Sigmoid)
+
         nc.vector.memset(scale_pool[:].bitcast(I32), 0)
         nc.vector.memset(bias_row[0:LAST, :].bitcast(I32), 0)
         ident = keep.tile([P, P], F32, name="ident", align_bytes=64)

@@ -23,13 +23,17 @@ QUADRANT = 32
 LAST = P - 1
 LANES = 16
 HALF = I // 2
+QUARTER = I // 4
 SLOT_TILES = HALF // P
 USER_TILES = Q // P
-PAIR_PIECES = [((256, 256),), ((256,), (128,), (64, 64))]
+VECTOR_BIASES = 384
 
-AT_WORDS1 = 0
-AT_RAW = 2 * HALF - 64
-AT_SPREAD = 2 * HALF
+AT_RAW = 0
+AT_WORDS = 0
+AT_COLUMNS1 = 1536
+AT_SPREAD = 2048
+AT_STAGED_LAST = AT_SPREAD + 4 * I
+AT_FIRST_DIFF = AT_STAGED_LAST - 2 * QUARTER
 
 
 def tile_attend_pairprefs_kernel(tc, query, item_words, item_scales, ib, offs, offs2, offs3, out):
@@ -65,91 +69,128 @@ def tile_attend_pairprefs_kernel(tc, query, item_words, item_scales, ib, offs, o
             nc.sync.dma_start(
                 scale_pool[r:P:QUADRANT, :].bitcast(I32), item_scales[0, r : D // QUADRANT : PACK, :].bitcast(I32)
             )
-        nc.sync.dma_start(word_pool[:].bitcast(I32), item_words[0].bitcast(I32))
         nc.sync.dma_start(q_raw[:], query.rearrange("(p t) q -> p t q", t=PACK))
+        nc.sync.dma_start(word_pool[:].bitcast(I32), item_words[0].bitcast(I32))
         nc.sync.dma_start(second_list[:], offs3)
         nc.sync.dma_start(first_list[:], offs2)
 
         def entries(tile, lo, hi):
             return tile[:, lo // LANES : hi // LANES]
 
-        columns = keep.tile([P, I // P], F32, name="columns", align_bytes=64)
+        def bank(tag, name):
+            return psum.tile([P, HALF], F32, name=name, tag=tag)
+
         biases = [keep.tile([P, HALF], F32, name="biases%d" % h, align_bytes=64) for h in range(2)]
+        nc.vector.tensor_copy(biases[0][:, 0:VECTOR_BIASES], bias_row[:].indirect(entries(slot_list, 0, VECTOR_BIASES)))
+        nc.scalar.activation(
+            biases[0][:, VECTOR_BIASES:HALF], bias_row[:].indirect(entries(slot_list, VECTOR_BIASES, HALF)), ACT.Copy
+        )
+        nc.scalar.activation(biases[1][:], bias_row[:].indirect(entries(slot_list, HALF, I)), ACT.Copy)
+
+        turned = [bank("turn%d" % h, "turned%d" % h) for h in range(2)]
         for h in range(2):
-            nc.scalar.activation(biases[h][:], bias_row[:].indirect(entries(slot_list, h * HALF, (h + 1) * HALF)), ACT.Copy)
-        spread_banks = []
-        for h in range(2):
-            turned = psum.tile([P, SLOT_TILES, P], F32, name="turned%d" % h, tag="turned%d" % h)
             for c in range(SLOT_TILES):
-                nc.tensor.transpose(turned[:, c, :], biases[h][:, c * P : (c + 1) * P], ident[:])
-            nc.scalar.copy(columns[:, h * SLOT_TILES : (h + 1) * SLOT_TILES], turned[:, :, LAST])
-            bank = psum.tile([P, SLOT_TILES, P], F32, name="spread_bank%d" % h, tag="spread%d" % h)
-            for c in range(SLOT_TILES):
-                k = h * SLOT_TILES + c
-                nc.tensor.transpose(bank[:, c, :], columns[:, k : k + 1].to_broadcast([P, P]), ident[:])
-            spread_banks.append(bank)
+                nc.tensor.transpose(turned[h][:, c * P : (c + 1) * P], biases[h][:, c * P : (c + 1) * P], ident[:])
+        columns = [
+            keep.tile([P, SLOT_TILES], F32, name="columns0", align_bytes=64),
+            reused.tile([P, SLOT_TILES], F32, name="columns1", align_bytes=64, offset=AT_COLUMNS1),
+        ]
+        nc.scalar.copy(columns[0][:], turned[0][:, LAST:HALF:P])
 
         grouped = keep.tile([P, Q, PACK], BF16, name="grouped", align_bytes=64)
         nc.scalar.copy(
             grouped[:].rearrange("p (c i) t -> p c t i", i=PACK),
             q_raw[:].rearrange("p t (c i) -> p c t i", i=PACK),
         )
-        spread = [
-            reused.tile([P, HALF], F32, name="spread%d" % h, align_bytes=64, offset=AT_SPREAD + 4 * HALF * h)
-            for h in range(2)
-        ]
+        nc.scalar.copy(columns[1][:], turned[1][:, LAST:HALF:P])
+
+        spread = []
         for h in range(2):
-            nc.scalar.copy(spread[h][:], spread_banks[h][:].rearrange("p c q -> p (c q)"))
+            spread_bank = bank("spread%d" % h, "spread_bank%d" % h)
+            for c in range(SLOT_TILES):
+                nc.tensor.transpose(
+                    spread_bank[:, c * P : (c + 1) * P], columns[h][:, c : c + 1].to_broadcast([P, P]), ident[:]
+                )
+            rows = reused.tile([P, HALF], F32, name="spread%d" % h, align_bytes=64, offset=AT_SPREAD + 4 * HALF * h)
+            nc.scalar.copy(rows[:], spread_bank[:])
+            spread.append(rows)
 
         scales = keep.tile([P, I], U8, name="scales", align_bytes=64)
-        words = [
-            keep.tile([P, HALF], U16, name="words0", align_bytes=64),
-            reused.tile([P, HALF], U16, name="words1", align_bytes=64, offset=AT_WORDS1),
+        words = [keep.tile([P, QUARTER], U16, name="words0", align_bytes=64)] + [
+            reused.tile([P, QUARTER], U16, name="words%d" % c, align_bytes=64, offset=AT_WORDS + 2 * QUARTER * (c - 1))
+            for c in range(1, 4)
         ]
         q_codes = keep.tile([P, Q], U32, name="q_codes", align_bytes=64)
         q_scales = keep.tile([P, Q], U8, name="q_scales", align_bytes=64)
 
+        def gather_words(c):
+            nc.vector.tensor_copy(words[c][:], word_pool[:].indirect(entries(slot_list, c * QUARTER, (c + 1) * QUARTER)))
+
         nc.vector.tensor_copy(scales[:], scale_pool[:].indirect(slot_list[:]))
-        nc.vector.tensor_copy(words[0][:], word_pool[:].indirect(entries(slot_list, 0, HALF)))
+        gather_words(0)
         nc.vector.quantize_mx(
             out=q_codes[:].bitcast(FP8X4), scales=q_scales[:], in_=grouped[:].rearrange("p q t -> p (q t)")
         )
-        nc.vector.tensor_copy(words[1][:], word_pool[:].indirect(entries(slot_list, HALF, I)))
+        for c in range(1, 4):
+            gather_words(c)
 
-        score = [keep.tile([P, I], F32, name="score%d" % ut, align_bytes=64) for ut in range(USER_TILES)]
-        products = {}
-        for h in range(2):
+        first_half = bank("a", "acc0_01")
+        products = {
+            (0, 0): first_half[:, 0:QUARTER],
+            (0, 1): first_half[:, QUARTER:HALF],
+            (0, 2): bank("b", "acc0_2")[:, 0:QUARTER],
+            (0, 3): bank("turn0", "acc0_3")[:, 0:QUARTER],
+            (1, 0): bank("c", "acc1_0")[:, 0:QUARTER],
+            (1, 1): bank("d", "acc1_1")[:, 0:QUARTER],
+            (1, 2): bank("turn1", "acc1_2")[:, 0:QUARTER],
+            (1, 3): bank("spread0", "acc1_3")[:, 0:QUARTER],
+        }
+        for c in range(4):
             for ut in range(USER_TILES):
                 users = slice(ut * P, (ut + 1) * P)
-                acc = psum.tile([P, HALF], F32, name="acc%d_%d" % (ut, h), tag="acc%d_%d" % (ut, h))
                 nc.tensor.matmul_mx(
-                    out=acc[:],
+                    out=products[ut, c],
                     lhsT=q_codes[:, users].bitcast(FP8X4),
                     lhsT_scale=q_scales[:, users],
-                    rhs=words[h][:].bitcast(FP4X4),
-                    rhs_scale=scales[:, h * HALF : (h + 1) * HALF],
+                    rhs=words[c][:].bitcast(FP4X4),
+                    rhs_scale=scales[:, c * QUARTER : (c + 1) * QUARTER],
                     start=True,
                     stop=True,
                 )
-                products[ut, h] = acc
-        for ut in range(USER_TILES):
-            for h in range(2):
-                nc.vector.tensor_tensor(score[ut][:, h * HALF : (h + 1) * HALF], products[ut, h][:], spread[h][:], ALU.add)
+
+        def spread_quarter(c):
+            return spread[c // 2][:, (c % 2) * QUARTER : (c % 2 + 1) * QUARTER]
+
+        score = [keep.tile([P, I], F32, name="score%d" % ut, align_bytes=64) for ut in range(USER_TILES)]
+        staged = [keep.tile([P, QUARTER], F32, name="staged%d" % c, align_bytes=64) for c in range(2)]
+        staged.append(reused.tile([P, QUARTER], F32, name="staged2", align_bytes=64, offset=AT_STAGED_LAST))
+        for c in range(3):
+            nc.scalar.copy(staged[c][:], products[1, c])
+            nc.gpsimd.tensor_tensor(score[1][:, c * QUARTER : (c + 1) * QUARTER], staged[c][:], spread_quarter(c), ALU.add)
+        nc.vector.tensor_tensor(score[0][:, 0:HALF], first_half[:], spread[0][:], ALU.add)
+        for ut, c in ((0, 2), (0, 3), (1, 3)):
+            nc.vector.tensor_tensor(
+                score[ut][:, c * QUARTER : (c + 1) * QUARTER], products[ut, c], spread_quarter(c), ALU.add
+            )
 
         second = [keep.tile([P, J], F32, name="second%d" % ut, align_bytes=64) for ut in range(USER_TILES)]
-        for ut in range(USER_TILES):
-            for lo in (0, J // 2):
-                nc.scalar.activation(
-                    second[ut][:, lo : lo + J // 2], score[ut][:].indirect(entries(second_list, lo, lo + J // 2)), ACT.Copy
-                )
-        for ut, stores in enumerate(PAIR_PIECES):
+        nc.scalar.activation(second[0][:, 0:256], score[0][:].indirect(entries(second_list, 0, 256)), ACT.Copy)
+        nc.vector.tensor_copy(second[0][:, 256:512], score[0][:].indirect(entries(second_list, 256, 512)))
+        for lo in (0, 256):
+            nc.scalar.activation(
+                second[1][:, lo : lo + 256], score[1][:].indirect(entries(second_list, lo, lo + 256)), ACT.Copy
+            )
+        for ut, stores in enumerate([((256,), (256,)), ((256,), (128,), (64, 64))]):
             result = keep.tile([P, J], F32, name="result%d" % ut, align_bytes=64)
             lo = 0
             for widths in stores:
                 stored = lo
                 for width in widths:
                     hi = lo + width
-                    diff = keep.tile([P, width], F32, name="diff%d_%d" % (ut, lo), align_bytes=64)
+                    if ut == 0 and lo == 0:
+                        diff = reused.tile([P, width], F32, name="diff0_0", align_bytes=64, offset=AT_FIRST_DIFF)
+                    else:
+                        diff = keep.tile([P, width], F32, name="diff%d_%d" % (ut, lo), align_bytes=64)
                     nc.vector.tensor_tensor(
                         diff[:], score[ut][:].indirect(entries(first_list, lo, hi)), second[ut][:, lo:hi], ALU.subtract
                     )

@@ -26,12 +26,11 @@ HALF = I // 2
 QUARTER = I // 4
 SLOT_TILES = HALF // P
 USER_TILES = Q // P
-VECTOR_BIASES = 384
+VECTOR_BIASES = 256
 
 AT_RAW = 0
 AT_WORDS = 0
-AT_COLUMNS1 = 1536
-AT_SPREAD = 2048
+AT_SPREAD = 4096
 AT_STAGED_LAST = AT_SPREAD + 4 * I
 AT_FIRST_DIFF = AT_STAGED_LAST - 2 * QUARTER
 
@@ -85,7 +84,10 @@ def tile_attend_pairprefs_kernel(tc, query, item_words, item_scales, ib, offs, o
         nc.scalar.activation(
             biases[0][:, VECTOR_BIASES:HALF], bias_row[:].indirect(entries(slot_list, VECTOR_BIASES, HALF)), ACT.Copy
         )
-        nc.scalar.activation(biases[1][:], bias_row[:].indirect(entries(slot_list, HALF, I)), ACT.Copy)
+        for lo, hi in ((HALF, I - P), (I - P, I)):
+            nc.scalar.activation(
+                biases[1][:, lo - HALF : hi - HALF], bias_row[:].indirect(entries(slot_list, lo, hi)), ACT.Copy
+            )
 
         turned = [bank("turn%d" % h, "turned%d" % h) for h in range(2)]
         for h in range(2):
@@ -93,15 +95,12 @@ def tile_attend_pairprefs_kernel(tc, query, item_words, item_scales, ib, offs, o
                 nc.tensor.transpose(turned[h][:, c * P : (c + 1) * P], biases[h][:, c * P : (c + 1) * P], ident[:])
         columns = [
             keep.tile([P, SLOT_TILES], F32, name="columns0", align_bytes=64),
-            reused.tile([P, SLOT_TILES], F32, name="columns1", align_bytes=64, offset=AT_COLUMNS1),
+            keep.tile([P, SLOT_TILES], F32, name="columns1", align_bytes=64),
         ]
         nc.scalar.copy(columns[0][:], turned[0][:, LAST:HALF:P])
 
         grouped = keep.tile([P, Q, PACK], BF16, name="grouped", align_bytes=64)
-        nc.scalar.copy(
-            grouped[:].rearrange("p (c i) t -> p c t i", i=PACK),
-            q_raw[:].rearrange("p t (c i) -> p c t i", i=PACK),
-        )
+        nc.gpsimd.tensor_scalar(grouped[:], q_raw[:].rearrange("p t q -> p q t"), 1.0, 0.0, ALU.mult, ALU.add)
         nc.scalar.copy(columns[1][:], turned[1][:, LAST:HALF:P])
 
         spread = []
@@ -146,7 +145,7 @@ def tile_attend_pairprefs_kernel(tc, query, item_words, item_scales, ib, offs, o
             (1, 3): bank("spread0", "acc1_3")[:, 0:QUARTER],
         }
         for c in range(4):
-            for ut in range(USER_TILES):
+            for ut in ((1, 0) if c < 2 else (0, 1)):
                 users = slice(ut * P, (ut + 1) * P)
                 nc.tensor.matmul_mx(
                     out=products[ut, c],

@@ -27,10 +27,11 @@ QUARTER = I // 4
 SLOT_TILES = HALF // P
 USER_TILES = Q // P
 VECTOR_BIASES = 256
+SCALAR_USERS = 128
 
 AT_RAW = 0
 AT_WORDS = 0
-AT_SPREAD = 4096
+AT_SPREAD = 2048
 AT_STAGED_LAST = AT_SPREAD + 4 * I
 AT_FIRST_DIFF = AT_STAGED_LAST - 2 * QUARTER
 
@@ -100,8 +101,19 @@ def tile_attend_pairprefs_kernel(tc, query, item_words, item_scales, ib, offs, o
         nc.scalar.copy(columns[0][:], turned[0][:, LAST:HALF:P])
 
         grouped = keep.tile([P, Q, PACK], BF16, name="grouped", align_bytes=64)
-        nc.gpsimd.tensor_scalar(grouped[:], q_raw[:].rearrange("p t q -> p q t"), 1.0, 0.0, ALU.mult, ALU.add)
         nc.scalar.copy(columns[1][:], turned[1][:, LAST:HALF:P])
+        nc.gpsimd.tensor_scalar(
+            grouped[:, SCALAR_USERS:Q, :],
+            q_raw[:, :, SCALAR_USERS:Q].rearrange("p t q -> p q t"),
+            1.0,
+            0.0,
+            ALU.mult,
+            ALU.add,
+        )
+        nc.scalar.copy(
+            grouped[:, 0:SCALAR_USERS, :].rearrange("p (c i) t -> p c t i", i=PACK),
+            q_raw[:, :, 0:SCALAR_USERS].rearrange("p t (c i) -> p c t i", i=PACK),
+        )
 
         spread = []
         for h in range(2):

@@ -22,18 +22,17 @@ PACK = 4
 QUADRANT = 32
 LAST = P - 1
 LANES = 16
-HALF = I // 2
+BLOCKS = D // 32
+PARKED = P - BLOCKS
+BANK = 512
 QUARTER = I // 4
-SLOT_TILES = HALF // P
 USER_TILES = Q // P
-VECTOR_BIASES = 256
-SCALAR_USERS = 128
+EARLY_SCALES = 3 * QUARTER
+VECTOR_SECONDS = 256
+VECTOR_CLEARS = 768
 
 AT_RAW = 0
-AT_WORDS = 0
-AT_SPREAD = 2048
-AT_STAGED_LAST = AT_SPREAD + 4 * I
-AT_FIRST_DIFF = AT_STAGED_LAST - 2 * QUARTER
+AT_LATE_WORDS = 0
 
 
 def tile_attend_pairprefs_kernel(tc, query, item_words, item_scales, ib, offs, offs2, offs3, out):
@@ -44,164 +43,160 @@ def tile_attend_pairprefs_kernel(tc, query, item_words, item_scales, ib, offs, o
         reused = ctx.enter_context(tc.tile_pool(name="reused", bufs=1))
         psum = ctx.enter_context(tc.psum_pool(name="psum", bufs=1))
 
+        def sbuf(name, width, dtype):
+            return keep.tile([P, width], dtype, name=name, align_bytes=64)
+
+        def bank(number, name):
+            return psum.tile([P, BANK], F32, name=name, tag="bank%d" % number)
+
+        def entries(tile, lo, hi):
+            return tile[:, lo // LANES : hi // LANES]
+
         slot_list = lists.tile([P, I // LANES], U16, name="slot_list")
         first_list = lists.tile([P, J // LANES], U16, name="first_list")
         second_list = lists.tile([P, J // LANES], U16, name="second_list")
-
-        scale_pool = keep.tile([P, T], U8, name="scale_pool", align_bytes=64)
-        word_pool = keep.tile([P, T], U16, name="word_pool", align_bytes=64)
-        bias_row = keep.tile([P, T], F32, name="bias_row", align_bytes=64)
+        scale_pool = sbuf("scale_pool", T, U8)
+        word_pool = sbuf("word_pool", T, U16)
+        bias_row = sbuf("bias_row", T, F32)
         q_raw = reused.tile([P, PACK, Q], F32, name="q_raw", align_bytes=64, offset=AT_RAW)
 
-        warm = keep.tile([P, 2], F32, name="warm", align_bytes=64)
+        warm = sbuf("warm", 2, F32)
         nc.gpsimd.memset(warm[:, 0:1], 0.0)
         nc.scalar.activation(warm[:, 1:2], warm[:, 0:1], ACT.Sigmoid)
 
-        nc.vector.memset(scale_pool[:].bitcast(I32), 0)
-        nc.vector.memset(bias_row[0:LAST, :].bitcast(I32), 0)
-        ident = keep.tile([P, P], F32, name="ident", align_bytes=64)
-        nc.vector.memset(ident[:], 0.0)
-        make_identity(nc, ident[:], nomemset=True)
-
-        nc.sync.dma_start(bias_row[LAST:P, :], ib[LAST:P, :])
+        nc.sync.dma_start(scale_pool[PARKED:P, :].bitcast(I32), item_scales[0].bitcast(I32))
         nc.sync.dma_start(slot_list[:], offs)
-        for r in range(PACK):
-            nc.sync.dma_start(
-                scale_pool[r:P:QUADRANT, :].bitcast(I32), item_scales[0, r : D // QUADRANT : PACK, :].bitcast(I32)
-            )
+        nc.sync.dma_start(bias_row[LAST:P, :], ib[LAST:P, :])
         nc.sync.dma_start(q_raw[:], query.rearrange("(p t) q -> p t q", t=PACK))
         nc.sync.dma_start(word_pool[:].bitcast(I32), item_words[0].bitcast(I32))
         nc.sync.dma_start(second_list[:], offs3)
         nc.sync.dma_start(first_list[:], offs2)
 
-        def entries(tile, lo, hi):
-            return tile[:, lo // LANES : hi // LANES]
+        scale_cuts = ((0, EARLY_SCALES), (EARLY_SCALES, I))
+        plane = sbuf("plane", I, U8)
+        ident = sbuf("ident", P, F32)
 
-        def bank(tag, name):
-            return psum.tile([P, HALF], F32, name=name, tag=tag)
+        def clear_on_vector(words):
+            cut = words.shape[1] // 2 - 1
+            nc.vector.memset(words[:, 0:cut], 0)
+            nc.vector.memset(words[:, cut:], 0)
 
-        biases = [keep.tile([P, HALF], F32, name="biases%d" % h, align_bytes=64) for h in range(2)]
-        nc.vector.tensor_copy(biases[0][:, 0:VECTOR_BIASES], bias_row[:].indirect(entries(slot_list, 0, VECTOR_BIASES)))
-        nc.scalar.activation(
-            biases[0][:, VECTOR_BIASES:HALF], bias_row[:].indirect(entries(slot_list, VECTOR_BIASES, HALF)), ACT.Copy
-        )
-        for lo, hi in ((HALF, I - P), (I - P, I)):
+        nc.gpsimd.memset(bias_row[0:LAST, VECTOR_CLEARS:T].bitcast(I32), 0)
+        clear_on_vector(bias_row[0:LAST, 0:VECTOR_CLEARS].bitcast(I32))
+        clear_on_vector(scale_pool[0:PARKED, :].bitcast(I32))
+        make_identity(nc, ident[:])
+        nc.gpsimd.memset(plane[:].bitcast(I32), 0)
+
+        for n, (lo, hi) in enumerate(scale_cuts):
+            parked = sbuf("parked%d" % n, hi - lo, U8)
+            nc.vector.tensor_copy(parked[:], scale_pool[:].indirect(entries(slot_list, lo, hi)))
+            for r in range(PACK):
+                nc.sync.dma_start(plane[r:P:QUADRANT, lo:hi].bitcast(I32), parked[PARKED + r : P : PACK, :].bitcast(I32))
+
+        tiles = QUARTER // P
+        biases = [keep.tile([P, QUARTER], F32, name="biases%d" % c, tag="biases%d" % (c % 2), align_bytes=64) for c in range(4)]
+        turned = [bank(c, "turned%d" % c) for c in range(4)]
+        columns = [sbuf("columns%d" % c, tiles, F32) for c in range(4)]
+        spread_banks = [bank(4 + c, "spread_bank%d" % c) for c in range(4)]
+        spread = sbuf("spread", I, F32)
+
+        def look_up_biases(c):
             nc.scalar.activation(
-                biases[1][:, lo - HALF : hi - HALF], bias_row[:].indirect(entries(slot_list, lo, hi)), ACT.Copy
+                biases[c][:], bias_row[:].indirect(entries(slot_list, c * QUARTER, (c + 1) * QUARTER)), ACT.Copy
             )
+            for k in range(tiles):
+                nc.tensor.transpose(turned[c][:, k * P : (k + 1) * P], biases[c][:, k * P : (k + 1) * P], ident[:])
 
-        turned = [bank("turn%d" % h, "turned%d" % h) for h in range(2)]
-        for h in range(2):
-            for c in range(SLOT_TILES):
-                nc.tensor.transpose(turned[h][:, c * P : (c + 1) * P], biases[h][:, c * P : (c + 1) * P], ident[:])
-        columns = [
-            keep.tile([P, SLOT_TILES], F32, name="columns0", align_bytes=64),
-            keep.tile([P, SLOT_TILES], F32, name="columns1", align_bytes=64),
-        ]
-        nc.scalar.copy(columns[0][:], turned[0][:, LAST:HALF:P])
+        def spread_biases(c):
+            nc.scalar.copy(columns[c][:], turned[c][:, LAST:QUARTER:P])
+            for k in range(tiles):
+                nc.tensor.transpose(
+                    spread_banks[c][:, k * P : (k + 1) * P], columns[c][:, k : k + 1].to_broadcast([P, P]), ident[:]
+                )
+
+        look_up_biases(0)
+        for c in range(1, 4):
+            look_up_biases(c)
+            spread_biases(c - 1)
+        spread_biases(3)
+        for c in range(4):
+            nc.scalar.copy(spread[:, c * QUARTER : (c + 1) * QUARTER], spread_banks[c][:, 0:QUARTER])
 
         grouped = keep.tile([P, Q, PACK], BF16, name="grouped", align_bytes=64)
-        nc.scalar.copy(columns[1][:], turned[1][:, LAST:HALF:P])
-        nc.gpsimd.tensor_scalar(
-            grouped[:, SCALAR_USERS:Q, :],
-            q_raw[:, :, SCALAR_USERS:Q].rearrange("p t q -> p q t"),
-            1.0,
-            0.0,
-            ALU.mult,
-            ALU.add,
-        )
-        nc.scalar.copy(
-            grouped[:, 0:SCALAR_USERS, :].rearrange("p (c i) t -> p c t i", i=PACK),
-            q_raw[:, :, 0:SCALAR_USERS].rearrange("p t (c i) -> p c t i", i=PACK),
-        )
+        nc.gpsimd.tensor_scalar(grouped[:], q_raw[:].rearrange("p t q -> p q t"), 1.0, 0.0, ALU.mult, ALU.add)
 
-        spread = []
-        for h in range(2):
-            spread_bank = bank("spread%d" % h, "spread_bank%d" % h)
-            for c in range(SLOT_TILES):
-                nc.tensor.transpose(
-                    spread_bank[:, c * P : (c + 1) * P], columns[h][:, c : c + 1].to_broadcast([P, P]), ident[:]
-                )
-            rows = reused.tile([P, HALF], F32, name="spread%d" % h, align_bytes=64, offset=AT_SPREAD + 4 * HALF * h)
-            nc.scalar.copy(rows[:], spread_bank[:])
-            spread.append(rows)
-
-        scales = keep.tile([P, I], U8, name="scales", align_bytes=64)
-        words = [keep.tile([P, QUARTER], U16, name="words0", align_bytes=64)] + [
-            reused.tile([P, QUARTER], U16, name="words%d" % c, align_bytes=64, offset=AT_WORDS + 2 * QUARTER * (c - 1))
-            for c in range(1, 4)
+        words = [sbuf("words%d" % c, QUARTER, U16) for c in range(2)] + [
+            reused.tile([P, QUARTER], U16, name="words%d" % c, align_bytes=64, offset=AT_LATE_WORDS + 2 * QUARTER * (c - 2))
+            for c in range(2, 4)
         ]
-        q_codes = keep.tile([P, Q], U32, name="q_codes", align_bytes=64)
-        q_scales = keep.tile([P, Q], U8, name="q_scales", align_bytes=64)
+        q_codes = sbuf("q_codes", Q, U32)
+        q_scales = sbuf("q_scales", Q, U8)
 
         def gather_words(c):
             nc.vector.tensor_copy(words[c][:], word_pool[:].indirect(entries(slot_list, c * QUARTER, (c + 1) * QUARTER)))
 
-        nc.vector.tensor_copy(scales[:], scale_pool[:].indirect(slot_list[:]))
         gather_words(0)
+        gather_words(1)
         nc.vector.quantize_mx(
             out=q_codes[:].bitcast(FP8X4), scales=q_scales[:], in_=grouped[:].rearrange("p q t -> p (q t)")
         )
-        for c in range(1, 4):
-            gather_words(c)
+        gather_words(2)
+        gather_words(3)
 
-        first_half = bank("a", "acc0_01")
+        front = bank(0, "front0")
+        back = bank(5, "back1")
         products = {
-            (0, 0): first_half[:, 0:QUARTER],
-            (0, 1): first_half[:, QUARTER:HALF],
-            (0, 2): bank("b", "acc0_2")[:, 0:QUARTER],
-            (0, 3): bank("turn0", "acc0_3")[:, 0:QUARTER],
-            (1, 0): bank("c", "acc1_0")[:, 0:QUARTER],
-            (1, 1): bank("d", "acc1_1")[:, 0:QUARTER],
-            (1, 2): bank("turn1", "acc1_2")[:, 0:QUARTER],
-            (1, 3): bank("spread0", "acc1_3")[:, 0:QUARTER],
+            (0, 0): front[:, 0:QUARTER],
+            (0, 1): front[:, QUARTER:BANK],
+            (1, 0): bank(1, "acc1_0")[:, 0:QUARTER],
+            (0, 2): bank(2, "acc0_2")[:, 0:QUARTER],
+            (1, 1): bank(3, "acc1_1")[:, 0:QUARTER],
+            (0, 3): bank(4, "acc0_3")[:, 0:QUARTER],
+            (1, 2): back[:, 0:QUARTER],
+            (1, 3): back[:, QUARTER:BANK],
         }
-        for c in range(4):
-            for ut in ((1, 0) if c < 2 else (0, 1)):
-                users = slice(ut * P, (ut + 1) * P)
-                nc.tensor.matmul_mx(
-                    out=products[ut, c],
-                    lhsT=q_codes[:, users].bitcast(FP8X4),
-                    lhsT_scale=q_scales[:, users],
-                    rhs=words[c][:].bitcast(FP4X4),
-                    rhs_scale=scales[:, c * QUARTER : (c + 1) * QUARTER],
-                    start=True,
-                    stop=True,
-                )
-
-        def spread_quarter(c):
-            return spread[c // 2][:, (c % 2) * QUARTER : (c % 2 + 1) * QUARTER]
-
-        score = [keep.tile([P, I], F32, name="score%d" % ut, align_bytes=64) for ut in range(USER_TILES)]
-        staged = [keep.tile([P, QUARTER], F32, name="staged%d" % c, align_bytes=64) for c in range(2)]
-        staged.append(reused.tile([P, QUARTER], F32, name="staged2", align_bytes=64, offset=AT_STAGED_LAST))
-        for c in range(3):
-            nc.scalar.copy(staged[c][:], products[1, c])
-            nc.gpsimd.tensor_tensor(score[1][:, c * QUARTER : (c + 1) * QUARTER], staged[c][:], spread_quarter(c), ALU.add)
-        nc.vector.tensor_tensor(score[0][:, 0:HALF], first_half[:], spread[0][:], ALU.add)
-        for ut, c in ((0, 2), (0, 3), (1, 3)):
-            nc.vector.tensor_tensor(
-                score[ut][:, c * QUARTER : (c + 1) * QUARTER], products[ut, c], spread_quarter(c), ALU.add
+        for ut, c in products:
+            users = slice(ut * P, (ut + 1) * P)
+            nc.tensor.matmul_mx(
+                out=products[ut, c],
+                lhsT=q_codes[:, users].bitcast(FP8X4),
+                lhsT_scale=q_scales[:, users],
+                rhs=words[c][:].bitcast(FP4X4),
+                rhs_scale=plane[:, c * QUARTER : (c + 1) * QUARTER],
+                start=True,
+                stop=True,
             )
 
-        second = [keep.tile([P, J], F32, name="second%d" % ut, align_bytes=64) for ut in range(USER_TILES)]
-        nc.scalar.activation(second[0][:, 0:256], score[0][:].indirect(entries(second_list, 0, 256)), ACT.Copy)
-        nc.vector.tensor_copy(second[0][:, 256:512], score[0][:].indirect(entries(second_list, 256, 512)))
+        def quarters(tile, lo, hi):
+            return tile[:, lo * QUARTER : hi * QUARTER]
+
+        score = [sbuf("score%d" % ut, I, F32) for ut in range(USER_TILES)]
+        for c in range(2):
+            staged = sbuf("staged%d" % c, QUARTER, F32)
+            nc.scalar.copy(staged[:], products[1, c])
+            nc.gpsimd.tensor_tensor(quarters(score[1], c, c + 1), staged[:], quarters(spread, c, c + 1), ALU.add)
+        nc.vector.tensor_tensor(quarters(score[0], 0, 2), front[:], quarters(spread, 0, 2), ALU.add)
+        for c in (2, 3):
+            nc.vector.tensor_tensor(quarters(score[0], c, c + 1), products[0, c], quarters(spread, c, c + 1), ALU.add)
+        nc.vector.tensor_tensor(quarters(score[1], 2, 4), back[:], quarters(spread, 2, 4), ALU.add)
+
+        second = [sbuf("second%d" % ut, J, F32) for ut in range(USER_TILES)]
+        own = J - VECTOR_SECONDS
+        for lo, hi in ((0, own),):
+            nc.scalar.activation(second[0][:, lo:hi], score[0][:].indirect(entries(second_list, lo, hi)), ACT.Copy)
+        nc.vector.tensor_copy(second[0][:, own:J], score[0][:].indirect(entries(second_list, own, J)))
         for lo in (0, 256):
             nc.scalar.activation(
                 second[1][:, lo : lo + 256], score[1][:].indirect(entries(second_list, lo, lo + 256)), ACT.Copy
             )
         for ut, stores in enumerate([((256,), (256,)), ((256,), (128,), (64, 64))]):
-            result = keep.tile([P, J], F32, name="result%d" % ut, align_bytes=64)
+            result = sbuf("result%d" % ut, J, F32)
             lo = 0
             for widths in stores:
                 stored = lo
                 for width in widths:
                     hi = lo + width
-                    if ut == 0 and lo == 0:
-                        diff = reused.tile([P, width], F32, name="diff0_0", align_bytes=64, offset=AT_FIRST_DIFF)
-                    else:
-                        diff = keep.tile([P, width], F32, name="diff%d_%d" % (ut, lo), align_bytes=64)
+                    diff = sbuf("diff%d_%d" % (ut, lo), width, F32)
                     nc.vector.tensor_tensor(
                         diff[:], score[ut][:].indirect(entries(first_list, lo, hi)), second[ut][:, lo:hi], ALU.subtract
                     )

@@ -27,9 +27,10 @@ PARKED = P - BLOCKS
 BANK = 512
 QUARTER = I // 4
 USER_TILES = Q // P
-EARLY_SCALES = 3 * QUARTER
+EARLY_SCALES = 2 * QUARTER
+VECTOR_BIASES = 128
+SCALAR_BIASES = ((0, 256), (256, 512), (640, 896), (896, 1024))
 VECTOR_SECONDS = 256
-VECTOR_CLEARS = 768
 
 AT_RAW = 0
 AT_LATE_WORDS = 0
@@ -64,9 +65,9 @@ def tile_attend_pairprefs_kernel(tc, query, item_words, item_scales, ib, offs, o
         nc.gpsimd.memset(warm[:, 0:1], 0.0)
         nc.scalar.activation(warm[:, 1:2], warm[:, 0:1], ACT.Sigmoid)
 
-        nc.sync.dma_start(scale_pool[PARKED:P, :].bitcast(I32), item_scales[0].bitcast(I32))
-        nc.sync.dma_start(slot_list[:], offs)
         nc.sync.dma_start(bias_row[LAST:P, :], ib[LAST:P, :])
+        nc.sync.dma_start(slot_list[:], offs)
+        nc.sync.dma_start(scale_pool[PARKED:P, :].bitcast(I32), item_scales[0].bitcast(I32))
         nc.sync.dma_start(q_raw[:], query.rearrange("(p t) q -> p t q", t=PACK))
         nc.sync.dma_start(word_pool[:].bitcast(I32), item_words[0].bitcast(I32))
         nc.sync.dma_start(second_list[:], offs3)
@@ -75,59 +76,51 @@ def tile_attend_pairprefs_kernel(tc, query, item_words, item_scales, ib, offs, o
         scale_cuts = ((0, EARLY_SCALES), (EARLY_SCALES, I))
         plane = sbuf("plane", I, U8)
         ident = sbuf("ident", P, F32)
+        nc.vector.memset(bias_row[0:LAST, :].bitcast(I32), 0)
+        nc.vector.memset(ident[:], 0.0)
+        make_identity(nc, ident[:], nomemset=True)
+        nc.vector.memset(scale_pool[0:PARKED, :].bitcast(I32), 0)
+        nc.vector.memset(plane[:].bitcast(I32), 0)
 
-        def clear_on_vector(words):
-            cut = words.shape[1] // 2 - 1
-            nc.vector.memset(words[:, 0:cut], 0)
-            nc.vector.memset(words[:, cut:], 0)
-
-        nc.gpsimd.memset(bias_row[0:LAST, VECTOR_CLEARS:T].bitcast(I32), 0)
-        clear_on_vector(bias_row[0:LAST, 0:VECTOR_CLEARS].bitcast(I32))
-        clear_on_vector(scale_pool[0:PARKED, :].bitcast(I32))
-        make_identity(nc, ident[:])
-        nc.gpsimd.memset(plane[:].bitcast(I32), 0)
-
-        for n, (lo, hi) in enumerate(scale_cuts):
+        def gather_scales(n):
+            lo, hi = scale_cuts[n]
             parked = sbuf("parked%d" % n, hi - lo, U8)
             nc.vector.tensor_copy(parked[:], scale_pool[:].indirect(entries(slot_list, lo, hi)))
             for r in range(PACK):
                 nc.sync.dma_start(plane[r:P:QUADRANT, lo:hi].bitcast(I32), parked[PARKED + r : P : PACK, :].bitcast(I32))
 
-        tiles = QUARTER // P
-        biases = [keep.tile([P, QUARTER], F32, name="biases%d" % c, tag="biases%d" % (c % 2), align_bytes=64) for c in range(4)]
-        turned = [bank(c, "turned%d" % c) for c in range(4)]
-        columns = [sbuf("columns%d" % c, tiles, F32) for c in range(4)]
-        spread_banks = [bank(4 + c, "spread_bank%d" % c) for c in range(4)]
-        spread = sbuf("spread", I, F32)
-
-        def look_up_biases(c):
+        biases = [sbuf("biases%d" % h, BANK, F32) for h in range(2)]
+        gather_scales(0)
+        nc.vector.tensor_copy(biases[1][:, 0:VECTOR_BIASES], bias_row[:].indirect(entries(slot_list, BANK, BANK + VECTOR_BIASES)))
+        gather_scales(1)
+        for lo, hi in SCALAR_BIASES:
+            h = lo // BANK
             nc.scalar.activation(
-                biases[c][:], bias_row[:].indirect(entries(slot_list, c * QUARTER, (c + 1) * QUARTER)), ACT.Copy
+                biases[h][:, lo - h * BANK : hi - h * BANK], bias_row[:].indirect(entries(slot_list, lo, hi)), ACT.Copy
             )
-            for k in range(tiles):
-                nc.tensor.transpose(turned[c][:, k * P : (k + 1) * P], biases[c][:, k * P : (k + 1) * P], ident[:])
 
-        def spread_biases(c):
-            nc.scalar.copy(columns[c][:], turned[c][:, LAST:QUARTER:P])
-            for k in range(tiles):
+        turned = [bank(h, "turned%d" % h) for h in range(2)]
+        for h in range(2):
+            for k in range(0, BANK, P):
+                nc.tensor.transpose(turned[h][:, k : k + P], biases[h][:, k : k + P], ident[:])
+        columns = [sbuf("columns%d" % h, BANK // P, F32) for h in range(2)]
+        for h in range(2):
+            nc.scalar.copy(columns[h][:], turned[h][:, LAST:BANK:P])
+        spread = sbuf("spread", I, F32)
+        for h in range(2):
+            spread_bank = bank(2 + h, "spread_bank%d" % h)
+            for k in range(BANK // P):
                 nc.tensor.transpose(
-                    spread_banks[c][:, k * P : (k + 1) * P], columns[c][:, k : k + 1].to_broadcast([P, P]), ident[:]
+                    spread_bank[:, k * P : (k + 1) * P], columns[h][:, k : k + 1].to_broadcast([P, P]), ident[:]
                 )
-
-        look_up_biases(0)
-        for c in range(1, 4):
-            look_up_biases(c)
-            spread_biases(c - 1)
-        spread_biases(3)
-        for c in range(4):
-            nc.scalar.copy(spread[:, c * QUARTER : (c + 1) * QUARTER], spread_banks[c][:, 0:QUARTER])
+            nc.scalar.copy(spread[:, h * BANK : (h + 1) * BANK], spread_bank[:])
 
         grouped = keep.tile([P, Q, PACK], BF16, name="grouped", align_bytes=64)
         nc.gpsimd.tensor_scalar(grouped[:], q_raw[:].rearrange("p t q -> p q t"), 1.0, 0.0, ALU.mult, ALU.add)
 
-        words = [sbuf("words%d" % c, QUARTER, U16) for c in range(2)] + [
-            reused.tile([P, QUARTER], U16, name="words%d" % c, align_bytes=64, offset=AT_LATE_WORDS + 2 * QUARTER * (c - 2))
-            for c in range(2, 4)
+        words = [sbuf("words0", QUARTER, U16)] + [
+            reused.tile([P, QUARTER], U16, name="words%d" % c, align_bytes=64, offset=AT_LATE_WORDS + 2 * QUARTER * (c - 1))
+            for c in range(1, 4)
         ]
         q_codes = sbuf("q_codes", Q, U32)
         q_scales = sbuf("q_scales", Q, U8)
@@ -136,25 +129,27 @@ def tile_attend_pairprefs_kernel(tc, query, item_words, item_scales, ib, offs, o
             nc.vector.tensor_copy(words[c][:], word_pool[:].indirect(entries(slot_list, c * QUARTER, (c + 1) * QUARTER)))
 
         gather_words(0)
-        gather_words(1)
         nc.vector.quantize_mx(
             out=q_codes[:].bitcast(FP8X4), scales=q_scales[:], in_=grouped[:].rearrange("p q t -> p (q t)")
         )
-        gather_words(2)
-        gather_words(3)
+        for c in range(1, 4):
+            gather_words(c)
 
-        front = bank(0, "front0")
-        back = bank(5, "back1")
+        front = bank(4, "front0")
         products = {
+            (1, 0): bank(5, "acc1_0")[:, 0:QUARTER],
             (0, 0): front[:, 0:QUARTER],
+            (1, 1): bank(6, "acc1_1")[:, 0:QUARTER],
             (0, 1): front[:, QUARTER:BANK],
-            (1, 0): bank(1, "acc1_0")[:, 0:QUARTER],
-            (0, 2): bank(2, "acc0_2")[:, 0:QUARTER],
-            (1, 1): bank(3, "acc1_1")[:, 0:QUARTER],
-            (0, 3): bank(4, "acc0_3")[:, 0:QUARTER],
-            (1, 2): back[:, 0:QUARTER],
-            (1, 3): back[:, QUARTER:BANK],
+            (0, 2): bank(7, "acc0_2")[:, 0:QUARTER],
+            (1, 2): bank(1, "acc1_2")[:, 0:QUARTER],
+            (0, 3): bank(0, "acc0_3")[:, 0:QUARTER],
+            (1, 3): bank(2, "acc1_3")[:, 0:QUARTER],
         }
+
+        def quarters(tile, lo, hi):
+            return tile[:, lo * QUARTER : hi * QUARTER]
+
         for ut, c in products:
             users = slice(ut * P, (ut + 1) * P)
             nc.tensor.matmul_mx(
@@ -162,23 +157,19 @@ def tile_attend_pairprefs_kernel(tc, query, item_words, item_scales, ib, offs, o
                 lhsT=q_codes[:, users].bitcast(FP8X4),
                 lhsT_scale=q_scales[:, users],
                 rhs=words[c][:].bitcast(FP4X4),
-                rhs_scale=plane[:, c * QUARTER : (c + 1) * QUARTER],
+                rhs_scale=quarters(plane, c, c + 1),
                 start=True,
                 stop=True,
             )
 
-        def quarters(tile, lo, hi):
-            return tile[:, lo * QUARTER : hi * QUARTER]
-
         score = [sbuf("score%d" % ut, I, F32) for ut in range(USER_TILES)]
-        for c in range(2):
+        for c in range(3):
             staged = sbuf("staged%d" % c, QUARTER, F32)
             nc.scalar.copy(staged[:], products[1, c])
             nc.gpsimd.tensor_tensor(quarters(score[1], c, c + 1), staged[:], quarters(spread, c, c + 1), ALU.add)
         nc.vector.tensor_tensor(quarters(score[0], 0, 2), front[:], quarters(spread, 0, 2), ALU.add)
-        for c in (2, 3):
-            nc.vector.tensor_tensor(quarters(score[0], c, c + 1), products[0, c], quarters(spread, c, c + 1), ALU.add)
-        nc.vector.tensor_tensor(quarters(score[1], 2, 4), back[:], quarters(spread, 2, 4), ALU.add)
+        for ut, c in ((0, 2), (0, 3), (1, 3)):
+            nc.vector.tensor_tensor(quarters(score[ut], c, c + 1), products[ut, c], quarters(spread, c, c + 1), ALU.add)
 
         second = [sbuf("second%d" % ut, J, F32) for ut in range(USER_TILES)]
         own = J - VECTOR_SECONDS

@@ -77,10 +77,10 @@ def tile_attend_pairprefs_kernel(tc, query, item_words, item_scales, ib, offs, o
         plane = sbuf("plane", I, U8)
         ident = sbuf("ident", P, F32)
         nc.vector.memset(bias_row[0:LAST, :].bitcast(I32), 0)
-        nc.vector.memset(ident[:], 0.0)
-        make_identity(nc, ident[:], nomemset=True)
         nc.vector.memset(scale_pool[0:PARKED, :].bitcast(I32), 0)
         nc.vector.memset(plane[:].bitcast(I32), 0)
+        nc.vector.memset(ident[:], 0.0)
+        make_identity(nc, ident[:], nomemset=True)
 
         def gather_scales(n):
             lo, hi = scale_cuts[n]
@@ -90,8 +90,8 @@ def tile_attend_pairprefs_kernel(tc, query, item_words, item_scales, ib, offs, o
                 nc.sync.dma_start(plane[r:P:QUADRANT, lo:hi].bitcast(I32), parked[PARKED + r : P : PACK, :].bitcast(I32))
 
         biases = [sbuf("biases%d" % h, BANK, F32) for h in range(2)]
-        gather_scales(0)
         nc.vector.tensor_copy(biases[1][:, 0:VECTOR_BIASES], bias_row[:].indirect(entries(slot_list, BANK, BANK + VECTOR_BIASES)))
+        gather_scales(0)
         gather_scales(1)
         for lo, hi in SCALAR_BIASES:
             h = lo // BANK

@@ -115,23 +115,29 @@ def tile_attend_pairprefs_kernel(tc, query, item_words, item_scales, ib, offs, o
                 )
             nc.scalar.copy(spread[:, h * BANK : (h + 1) * BANK], spread_bank[:])
 
-        grouped = keep.tile([P, Q, PACK], BF16, name="grouped", align_bytes=64)
-        nc.gpsimd.tensor_scalar(grouped[:], q_raw[:].rearrange("p t q -> p q t"), 1.0, 0.0, ALU.mult, ALU.add)
+        grouped = [keep.tile([P, P, PACK], BF16, name="grouped%d" % ut, align_bytes=64) for ut in range(USER_TILES)]
+        for ut in (1, 0):
+            raw = q_raw[:, :, ut * P : (ut + 1) * P].rearrange("p t q -> p q t")
+            nc.gpsimd.tensor_scalar(grouped[ut][:], raw, 1.0, 0.0, ALU.mult, ALU.add)
 
         words = [sbuf("words0", QUARTER, U16)] + [
             reused.tile([P, QUARTER], U16, name="words%d" % c, align_bytes=64, offset=AT_LATE_WORDS + 2 * QUARTER * (c - 1))
             for c in range(1, 4)
         ]
-        q_codes = sbuf("q_codes", Q, U32)
-        q_scales = sbuf("q_scales", Q, U8)
+        q_codes = [sbuf("q_codes%d" % ut, P, U32) for ut in range(USER_TILES)]
+        q_scales = [sbuf("q_scales%d" % ut, P, U8) for ut in range(USER_TILES)]
 
         def gather_words(c):
             nc.vector.tensor_copy(words[c][:], word_pool[:].indirect(entries(slot_list, c * QUARTER, (c + 1) * QUARTER)))
 
+        def quantise(ut):
+            nc.vector.quantize_mx(
+                out=q_codes[ut][:].bitcast(FP8X4), scales=q_scales[ut][:], in_=grouped[ut][:].rearrange("p q t -> p (q t)")
+            )
+
+        quantise(1)
         gather_words(0)
-        nc.vector.quantize_mx(
-            out=q_codes[:].bitcast(FP8X4), scales=q_scales[:], in_=grouped[:].rearrange("p q t -> p (q t)")
-        )
+        quantise(0)
         for c in range(1, 4):
             gather_words(c)
 
@@ -151,11 +157,10 @@ def tile_attend_pairprefs_kernel(tc, query, item_words, item_scales, ib, offs, o
             return tile[:, lo * QUARTER : hi * QUARTER]
 
         for ut, c in products:
-            users = slice(ut * P, (ut + 1) * P)
             nc.tensor.matmul_mx(
                 out=products[ut, c],
-                lhsT=q_codes[:, users].bitcast(FP8X4),
-                lhsT_scale=q_scales[:, users],
+                lhsT=q_codes[ut][:].bitcast(FP8X4),
+                lhsT_scale=q_scales[ut][:],
                 rhs=words[c][:].bitcast(FP4X4),
                 rhs_scale=quarters(plane, c, c + 1),
                 start=True,

@@ -30,7 +30,7 @@ USER_TILES = Q // P
 EARLY_SCALES = 2 * QUARTER
 VECTOR_BIASES = 128
 SCALAR_BIASES = ((0, 256), (256, 512), (640, 896), (896, 1024))
-VECTOR_SECONDS = 256
+VECTOR_SECONDS = 128
 
 AT_RAW = 0
 AT_LATE_WORDS = 0
@@ -77,10 +77,9 @@ def tile_attend_pairprefs_kernel(tc, query, item_words, item_scales, ib, offs, o
         plane = sbuf("plane", I, U8)
         ident = sbuf("ident", P, F32)
         nc.vector.memset(bias_row[0:LAST, :].bitcast(I32), 0)
-        nc.vector.memset(scale_pool[0:PARKED, :].bitcast(I32), 0)
-        nc.vector.memset(plane[:].bitcast(I32), 0)
-        nc.vector.memset(ident[:], 0.0)
-        make_identity(nc, ident[:], nomemset=True)
+        nc.gpsimd.memset(scale_pool[0:PARKED, :].bitcast(I32), 0)
+        make_identity(nc, ident[:])
+        nc.gpsimd.memset(plane[:].bitcast(I32), 0)
 
         def gather_scales(n):
             lo, hi = scale_cuts[n]
@@ -142,15 +141,16 @@ def tile_attend_pairprefs_kernel(tc, query, item_words, item_scales, ib, offs, o
             gather_words(c)
 
         front = bank(4, "front0")
+        back = bank(1, "back1")
         products = {
             (1, 0): bank(5, "acc1_0")[:, 0:QUARTER],
             (0, 0): front[:, 0:QUARTER],
             (1, 1): bank(6, "acc1_1")[:, 0:QUARTER],
             (0, 1): front[:, QUARTER:BANK],
             (0, 2): bank(7, "acc0_2")[:, 0:QUARTER],
-            (1, 2): bank(1, "acc1_2")[:, 0:QUARTER],
             (0, 3): bank(0, "acc0_3")[:, 0:QUARTER],
-            (1, 3): bank(2, "acc1_3")[:, 0:QUARTER],
+            (1, 2): back[:, 0:QUARTER],
+            (1, 3): back[:, QUARTER:BANK],
         }
 
         def quarters(tile, lo, hi):
@@ -168,17 +168,18 @@ def tile_attend_pairprefs_kernel(tc, query, item_words, item_scales, ib, offs, o
             )
 
         score = [sbuf("score%d" % ut, I, F32) for ut in range(USER_TILES)]
-        for c in range(3):
+        for c in range(2):
             staged = sbuf("staged%d" % c, QUARTER, F32)
             nc.scalar.copy(staged[:], products[1, c])
             nc.gpsimd.tensor_tensor(quarters(score[1], c, c + 1), staged[:], quarters(spread, c, c + 1), ALU.add)
         nc.vector.tensor_tensor(quarters(score[0], 0, 2), front[:], quarters(spread, 0, 2), ALU.add)
-        for ut, c in ((0, 2), (0, 3), (1, 3)):
-            nc.vector.tensor_tensor(quarters(score[ut], c, c + 1), products[ut, c], quarters(spread, c, c + 1), ALU.add)
+        for c in (2, 3):
+            nc.vector.tensor_tensor(quarters(score[0], c, c + 1), products[0, c], quarters(spread, c, c + 1), ALU.add)
+        nc.vector.tensor_tensor(quarters(score[1], 2, 4), back[:], quarters(spread, 2, 4), ALU.add)
 
         second = [sbuf("second%d" % ut, J, F32) for ut in range(USER_TILES)]
         own = J - VECTOR_SECONDS
-        for lo, hi in ((0, own),):
+        for lo, hi in ((0, 256), (256, own)):
             nc.scalar.activation(second[0][:, lo:hi], score[0][:].indirect(entries(second_list, lo, hi)), ACT.Copy)
         nc.vector.tensor_copy(second[0][:, own:J], score[0][:].indirect(entries(second_list, own, J)))
         for lo in (0, 256):

@@ -77,9 +77,10 @@ def tile_attend_pairprefs_kernel(tc, query, item_words, item_scales, ib, offs, o
         plane = sbuf("plane", I, U8)
         ident = sbuf("ident", P, F32)
         nc.vector.memset(bias_row[0:LAST, :].bitcast(I32), 0)
-        nc.gpsimd.memset(scale_pool[0:PARKED, :].bitcast(I32), 0)
-        make_identity(nc, ident[:])
-        nc.gpsimd.memset(plane[:].bitcast(I32), 0)
+        nc.vector.memset(scale_pool[0:PARKED, :].bitcast(I32), 0)
+        nc.vector.memset(plane[:].bitcast(I32), 0)
+        nc.vector.memset(ident[:], 0.0)
+        make_identity(nc, ident[:], nomemset=True)
 
         def gather_scales(n):
             lo, hi = scale_cuts[n]

from contextlib import ExitStack

import concourse.mybir as mybir
from concourse.masks import make_identity

D, T, I, J, Q = 512, 2048, 1024, 512, 256
FLOPS = 2 * D * I * Q

F32 = mybir.dt.float32
BF16 = mybir.dt.bfloat16
I32 = mybir.dt.int32
U32 = mybir.dt.uint32
U16 = mybir.dt.uint16
U8 = mybir.dt.uint8
FP8X4 = mybir.dt.float8_e4m3fn_x4
FP4X4 = mybir.dt.float4_e2m1fn_x4
ACT = mybir.ActivationFunctionType
ALU = mybir.AluOpType

P = 128
PACK = 4
QUADRANT = 32
LAST = P - 1
LANES = 16
BLOCKS = D // 32
PARKED = P - BLOCKS
BANK = 512
QUARTER = I // 4
USER_TILES = Q // P
EARLY_SCALES = 2 * QUARTER
VECTOR_BIASES = 128
SCALAR_BIASES = ((0, 256), (256, 512), (640, 896), (896, 1024))
VECTOR_SECONDS = 128

AT_RAW = 0
AT_LATE_WORDS = 0


def tile_attend_pairprefs_kernel(tc, query, item_words, item_scales, ib, offs, offs2, offs3, out):
    nc = tc.nc
    with ExitStack() as ctx:
        lists = ctx.enter_context(tc.tile_pool(name="lists", bufs=1))
        keep = ctx.enter_context(tc.tile_pool(name="keep", bufs=1))
        reused = ctx.enter_context(tc.tile_pool(name="reused", bufs=1))
        psum = ctx.enter_context(tc.psum_pool(name="psum", bufs=1))

        def sbuf(name, width, dtype):
            return keep.tile([P, width], dtype, name=name, align_bytes=64)

        def bank(number, name):
            return psum.tile([P, BANK], F32, name=name, tag="bank%d" % number)

        def entries(tile, lo, hi):
            return tile[:, lo // LANES : hi // LANES]

        slot_list = lists.tile([P, I // LANES], U16, name="slot_list")
        first_list = lists.tile([P, J // LANES], U16, name="first_list")
        second_list = lists.tile([P, J // LANES], U16, name="second_list")
        scale_pool = sbuf("scale_pool", T, U8)
        word_pool = sbuf("word_pool", T, U16)
        bias_row = sbuf("bias_row", T, F32)
        q_raw = reused.tile([P, PACK, Q], F32, name="q_raw", align_bytes=64, offset=AT_RAW)

        warm = sbuf("warm", 2, F32)
        nc.gpsimd.memset(warm[:, 0:1], 0.0)
        nc.scalar.activation(warm[:, 1:2], warm[:, 0:1], ACT.Sigmoid)

        nc.sync.dma_start(bias_row[LAST:P, :], ib[LAST:P, :])
        nc.sync.dma_start(slot_list[:], offs)
        nc.sync.dma_start(scale_pool[PARKED:P, :].bitcast(I32), item_scales[0].bitcast(I32))
        nc.sync.dma_start(q_raw[:], query.rearrange("(p t) q -> p t q", t=PACK))
        nc.sync.dma_start(word_pool[:].bitcast(I32), item_words[0].bitcast(I32))
        nc.sync.dma_start(second_list[:], offs3)
        nc.sync.dma_start(first_list[:], offs2)

        scale_cuts = ((0, EARLY_SCALES), (EARLY_SCALES, I))
        plane = sbuf("plane", I, U8)
        ident = sbuf("ident", P, F32)
        nc.vector.memset(bias_row[0:LAST, :].bitcast(I32), 0)
        nc.vector.memset(scale_pool[0:PARKED, :].bitcast(I32), 0)
        nc.vector.memset(plane[:].bitcast(I32), 0)
        nc.vector.memset(ident[:], 0.0)
        make_identity(nc, ident[:], nomemset=True)

        def gather_scales(n):
            lo, hi = scale_cuts[n]
            parked = sbuf("parked%d" % n, hi - lo, U8)
            nc.vector.tensor_copy(parked[:], scale_pool[:].indirect(entries(slot_list, lo, hi)))
            for r in range(PACK):
                nc.sync.dma_start(plane[r:P:QUADRANT, lo:hi].bitcast(I32), parked[PARKED + r : P : PACK, :].bitcast(I32))

        biases = [sbuf("biases%d" % h, BANK, F32) for h in range(2)]
        nc.vector.tensor_copy(biases[1][:, 0:VECTOR_BIASES], bias_row[:].indirect(entries(slot_list, BANK, BANK + VECTOR_BIASES)))
        gather_scales(0)
        gather_scales(1)
        for lo, hi in SCALAR_BIASES:
            h = lo // BANK
            nc.scalar.activation(
                biases[h][:, lo - h * BANK : hi - h * BANK], bias_row[:].indirect(entries(slot_list, lo, hi)), ACT.Copy
            )

        turned = [bank(h, "turned%d" % h) for h in range(2)]
        for h in range(2):
            for k in range(0, BANK, P):
                nc.tensor.transpose(turned[h][:, k : k + P], biases[h][:, k : k + P], ident[:])
        columns = [sbuf("columns%d" % h, BANK // P, F32) for h in range(2)]
        for h in range(2):
            nc.scalar.copy(columns[h][:], turned[h][:, LAST:BANK:P])
        spread = sbuf("spread", I, F32)
        for h in range(2):
            spread_bank = bank(2 + h, "spread_bank%d" % h)
            for k in range(BANK // P):
                nc.tensor.transpose(
                    spread_bank[:, k * P : (k + 1) * P], columns[h][:, k : k + 1].to_broadcast([P, P]), ident[:]
                )
            nc.scalar.copy(spread[:, h * BANK : (h + 1) * BANK], spread_bank[:])

        grouped = [keep.tile([P, P, PACK], BF16, name="grouped%d" % ut, align_bytes=64) for ut in range(USER_TILES)]
        for ut in (1, 0):
            raw = q_raw[:, :, ut * P : (ut + 1) * P].rearrange("p t q -> p q t")
            nc.gpsimd.tensor_scalar(grouped[ut][:], raw, 1.0, 0.0, ALU.mult, ALU.add)

        words = [sbuf("words0", QUARTER, U16)] + [
            reused.tile([P, QUARTER], U16, name="words%d" % c, align_bytes=64, offset=AT_LATE_WORDS + 2 * QUARTER * (c - 1))
            for c in range(1, 4)
        ]
        q_codes = [sbuf("q_codes%d" % ut, P, U32) for ut in range(USER_TILES)]
        q_scales = [sbuf("q_scales%d" % ut, P, U8) for ut in range(USER_TILES)]

        def gather_words(c):
            nc.vector.tensor_copy(words[c][:], word_pool[:].indirect(entries(slot_list, c * QUARTER, (c + 1) * QUARTER)))

        def quantise(ut):
            nc.vector.quantize_mx(
                out=q_codes[ut][:].bitcast(FP8X4), scales=q_scales[ut][:], in_=grouped[ut][:].rearrange("p q t -> p (q t)")
            )

        quantise(1)
        gather_words(0)
        quantise(0)
        for c in range(1, 4):
            gather_words(c)

        front = bank(4, "front0")
        back = bank(1, "back1")
        products = {
            (1, 0): bank(5, "acc1_0")[:, 0:QUARTER],
            (0, 0): front[:, 0:QUARTER],
            (1, 1): bank(6, "acc1_1")[:, 0:QUARTER],
            (0, 1): front[:, QUARTER:BANK],
            (0, 2): bank(7, "acc0_2")[:, 0:QUARTER],
            (0, 3): bank(0, "acc0_3")[:, 0:QUARTER],
            (1, 2): back[:, 0:QUARTER],
            (1, 3): back[:, QUARTER:BANK],
        }

        def quarters(tile, lo, hi):
            return tile[:, lo * QUARTER : hi * QUARTER]

        for ut, c in products:
            nc.tensor.matmul_mx(
                out=products[ut, c],
                lhsT=q_codes[ut][:].bitcast(FP8X4),
                lhsT_scale=q_scales[ut][:],
                rhs=words[c][:].bitcast(FP4X4),
                rhs_scale=quarters(plane, c, c + 1),
                start=True,
                stop=True,
            )

        score = [sbuf("score%d" % ut, I, F32) for ut in range(USER_TILES)]
        for c in range(2):
            staged = sbuf("staged%d" % c, QUARTER, F32)
            nc.scalar.copy(staged[:], products[1, c])
            nc.gpsimd.tensor_tensor(quarters(score[1], c, c + 1), staged[:], quarters(spread, c, c + 1), ALU.add)
        nc.vector.tensor_tensor(quarters(score[0], 0, 2), front[:], quarters(spread, 0, 2), ALU.add)
        for c in (2, 3):
            nc.vector.tensor_tensor(quarters(score[0], c, c + 1), products[0, c], quarters(spread, c, c + 1), ALU.add)
        nc.vector.tensor_tensor(quarters(score[1], 2, 4), back[:], quarters(spread, 2, 4), ALU.add)

        second = [sbuf("second%d" % ut, J, F32) for ut in range(USER_TILES)]
        own = J - VECTOR_SECONDS
        for lo, hi in ((0, 256), (256, own)):
            nc.scalar.activation(second[0][:, lo:hi], score[0][:].indirect(entries(second_list, lo, hi)), ACT.Copy)
        nc.vector.tensor_copy(second[0][:, own:J], score[0][:].indirect(entries(second_list, own, J)))
        for lo in (0, 256):
            nc.scalar.activation(
                second[1][:, lo : lo + 256], score[1][:].indirect(entries(second_list, lo, lo + 256)), ACT.Copy
            )
        for ut, stores in enumerate([((256,), (256,)), ((256,), (128,), (64, 64))]):
            result = sbuf("result%d" % ut, J, F32)
            lo = 0
            for widths in stores:
                stored = lo
                for width in widths:
                    hi = lo + width
                    diff = sbuf("diff%d_%d" % (ut, lo), width, F32)
                    nc.vector.tensor_tensor(
                        diff[:], score[ut][:].indirect(entries(first_list, lo, hi)), second[ut][:, lo:hi], ALU.subtract
                    )
                    nc.scalar.activation(result[:, lo:hi], diff[:], ACT.Sigmoid)
                    lo = hi
                nc.sync.dma_start(out[ut * P : (ut + 1) * P, stored:lo], result[:, stored:lo])
